import numpy as np
import ml_dtypes


def mxq(x, axis, fmt="e4m3"):
    dtype, down = {"e4m3": (ml_dtypes.float8_e4m3fn, 7), "e5m2": (ml_dtypes.float8_e5m2, 14)}[fmt]
    v = np.moveaxis(np.asarray(x, np.float32).astype(ml_dtypes.bfloat16).astype(np.float64), axis, -1)
    blocks = v.reshape(v.shape[:-1] + (-1, 32))
    amax = np.abs(blocks).max(-1, keepdims=True)
    byte = np.maximum(np.where(amax > 0, np.frexp(amax)[1] - 1 + 127, 0) - down, 1)
    scale = np.exp2(byte - 127.0)
    codes = (blocks / scale).astype(np.float32).astype(dtype).astype(np.float64)
    return np.moveaxis((codes * scale).reshape(v.shape), -1, axis)


WIDE = False


def mx_kscale(k):
    if not WIDE:
        return np.ones(k)
    levels = np.array([18, -18])
    if k % 512:
        return np.exp2(np.random.permutation(np.resize(levels, k // 32))).repeat(32)
    a = np.empty((k // 512, 16))
    for p in range(k // 512):
        a[p, :8] = np.random.permutation(np.resize(levels, 8))
        for g in range(8):
            far = levels[np.abs(levels - a[p, g]) >= 10]
            a[p, g + 8] = far[np.random.randint(len(far))]
    return np.exp2(a.ravel()).repeat(32)


def f64(x):
    return np.asarray(x).astype(np.float64)


def striped(idx):
    return np.tile(np.asarray(idx).reshape(-1, 16).T, (8, 1)).astype(np.uint16)


def unstriped(offs):
    return offs[:16].T.reshape(-1).astype(np.int64)

def planes(y):
    n, m = y.shape
    v = y.astype(np.float32).astype(ml_dtypes.bfloat16).astype(np.float64).reshape(n // 32, 32, m)
    top = np.abs(v).max(1)
    byte = np.clip(np.where(top > 0, np.frexp(top)[1] - 1 + 127 - 7, 1), 1, 254)
    codes = (v * np.exp2(127.0 - byte)[:, None, :]).reshape(n, m).astype(np.float32).astype(ml_dtypes.float8_e4m3fn).view(np.uint8)
    words = codes.reshape(n // 512, 128, 4, m).transpose(0, 1, 3, 2)
    return np.ascontiguousarray(words), np.ascontiguousarray(byte.astype(np.uint8).reshape(n // 512, 16, m))


def setup_inputs():
    n = np.random.standard_normal
    uni = np.random.uniform
    idx = np.random.permutation(2048)[:512]
    jdx = np.random.permutation(2048)[:512]
    f_d = mx_kscale(512)
    f_j = np.ones(2048)
    f_j[jdx] = mx_kscale(512)
    return {
        "uT": (n((512, 2048)) / np.sqrt(512) * f_d[:, None]).astype(np.float32),
        "vT": (n((512, 2048)) / f_d[:, None] * f_j[None, :]).astype(np.float32),
        "su": np.tile(uni(0.75, 1.3, 2048), (128, 1)).astype(np.float32),
        "sv": np.tile(uni(0.75, 1.3, 2048) / f_j, (128, 1)).astype(np.float32),
        "y": (0.5 * n((512, 512)) + n((512, 1)) + n((1, 512))).astype(np.float32),
        "offs": striped(idx),
        "qoffs": striped(jdx),
    }


def reference(uT, vT, su, sv, y, offs, qoffs):
    idx = unstriped(offs)
    jdx = unstriped(qoffs)
    uT_i = f64(uT)[:, idx]
    vT_j = f64(vT)[:, jdx]
    su_i = f64(su)[:1][:, idx]
    sv_j = f64(sv)[:1][:, jdx]
    suc = su_i.T
    a = mxq(uT_i, 0, "e4m3").T @ mxq(vT_j, 0, "e4m3")
    b = suc * sv_j * a - f64(y)
    r1 = (b).sum(-1, keepdims=True)
    c = b - r1 / 512.0
    ct = c.T
    c1 = (ct).sum(-1, keepdims=True)
    cr = c1.T
    g = suc * sv_j * (c - cr / 512.0)
    du = mxq(vT_j, 1, "e4m3") @ mxq(g, 1, "e5m2").T
    out_0 = np.zeros((512, 2048))
    out_0[:, idx] = du
    return (out_0,) + planes(out_0)

@@ -1,0 +1,254 @@
+from contextlib import ExitStack
+
+import concourse.mybir as mybir
+from concourse.masks import make_identity
+
+F32 = mybir.dt.float32
+BF16 = mybir.dt.bfloat16
+U32 = mybir.dt.uint32
+I32 = mybir.dt.int32
+U16 = mybir.dt.uint16
+U8 = mybir.dt.uint8
+E4M3 = mybir.dt.float8_e4m3fn_x4
+E5M2 = mybir.dt.float8_e5m2_x4
+ACT = mybir.ActivationFunctionType
+ALU = mybir.AluOpType
+
+P = 128
+PACK = 4
+N = 512
+T = 2048
+CHUNKS = 4
+CW = T // CHUNKS
+
+FLOPS = 2 * 2 * 512 * 512 * 512
+
+
+def tile_attend_gcentre_pl_kernel(tc, uT, vT, su, sv, y, offs, qoffs, out_0, out_1, out_2):
+    nc = tc.nc
+    with ExitStack() as ctx:
+        held = ctx.enter_context(tc.tile_pool(name="held", bufs=1))
+        sb = ctx.enter_context(tc.tile_pool(name="sb", bufs=1))
+        psum = ctx.enter_context(tc.psum_pool(name="psum", bufs=1))
+
+        def tile(shape, dtype, name, tag=None):
+            return sb.tile(shape, dtype, name=name, tag=tag or name, align_bytes=64)
+
+        def bank(name, tag):
+            return psum.tile([P, N], F32, name=name, tag=tag)
+
+        item_list = held.tile([P, N // 16], U16, name="item_list")
+        partner_list = held.tile([P, N // 16], U16, name="partner_list")
+        nc.sync.dma_start(partner_list[:], qoffs)
+        nc.sync.dma_start(item_list[:], offs)
+
+        u_rows = uT.rearrange("(p t) c -> p t c", t=PACK)
+        v_rows = vT.rearrange("(p t) c -> p t c", t=PACK)
+        v_win = [tile([P, T], F32, "v_win%d" % t) for t in range(PACK)]
+        u_win = [tile([P, T], F32, "u_win%d" % t) for t in range(PACK)]
+        y_sb = [tile([P, N], F32, "y_sb%d" % q) for q in range(PACK)]
+        su_win = tile([P, T], F32, "su_win")
+        sv_win = tile([P, T], F32, "sv_win")
+        RUN = T // P
+        sv_run = tile([P, RUN], F32, "sv_run")
+        su_run = tile([P, RUN], F32, "su_run")
+        nc.sync.dma_start(sv_run[:], sv[0].rearrange("(p k) -> p k", k=RUN))
+        nc.sync.dma_start(su_run[:], su[0].rearrange("(p k) -> p k", k=RUN))
+        for t in range(PACK):
+            nc.sync.dma_start(v_win[t][:], v_rows[:, t, :])
+        for t in range(PACK):
+            nc.sync.dma_start(u_win[t][:], u_rows[:, t, :])
+        for q in range(PACK):
+            nc.sync.dma_start(y_sb[q][:], y[q * P : (q + 1) * P, :])
+
+        ident = tile([P, P], F32, "ident")
+        make_identity(nc, ident[:])
+        out_win = [tile([P, T], F32, "out_win%d" % t) for t in range(PACK)]
+        for t in range(PACK):
+            nc.gpsimd.memset(out_win[t][:], 0.0)
+
+        for run, win, tagc in ((sv_run, sv_win, "A"), (su_run, su_win, "C")):
+            for bk in range(PACK):
+                sp = bank("spread%s%d" % (tagc, bk), "%s%d" % (tagc, bk))
+                for k in range(PACK):
+                    col = PACK * bk + k
+                    nc.tensor.transpose(sp[:, k * P : (k + 1) * P], run[:, col : col + 1].to_broadcast([P, P]), ident[:])
+                nc.scalar.copy(
+                    win[:].rearrange("m (p k) -> m p k", k=RUN)[:, :, PACK * bk : PACK * (bk + 1)],
+                    sp[:].rearrange("m (k p) -> m p k", k=PACK),
+                )
+
+        v_g = tile([P, PACK, N], BF16, "v_g")
+        s_g = tile([P, N], F32, "s_g")
+        t_g = tile([P, N], F32, "t_g")
+        for t in range(PACK):
+            nc.vector.tensor_copy(v_g[:, t, :], v_win[t][:].indirect(partner_list[:]))
+            if t == 1:
+                nc.vector.tensor_copy(t_g[:], sv_win[:].indirect(partner_list[:]))
+            if t == 2:
+                nc.vector.tensor_copy(s_g[:], su_win[:].indirect(item_list[:]))
+
+        t_row = tile([P, N], F32, "t_row")
+        nc.scalar.copy(t_row[:].rearrange("p (r s) -> p r s", r=PACK), t_g[:].rearrange("p (s r) -> p r s", r=PACK))
+        t_ps = bank("t_ps", "A2")
+        s_ps = bank("s_ps", "A3")
+        for r in range(PACK):
+            nc.tensor.transpose(t_ps[:, r * P : (r + 1) * P], t_row[:, r * P : (r + 1) * P], ident[:])
+        for q in range(PACK):
+            nc.tensor.transpose(s_ps[:, q * P : (q + 1) * P], s_g[:, q * P : (q + 1) * P], ident[:])
+        t_col = tile([P, PACK], F32, "t_col")
+        s_col = tile([P, PACK], F32, "s_col")
+        nc.scalar.copy(t_col[:], t_ps[:, 0:N:P])
+        nc.scalar.copy(s_col[:], s_ps[:, 0:N:P])
+        w = [tile([P, N], F32, "w%d" % r) for r in range(PACK)]
+        for r in range(PACK):
+            nc.scalar.activation(w[r][:], s_g[:], ACT.Copy, scale=t_col[:, r : r + 1])
+
+        v_d = tile([P, N, PACK], BF16, "v_d")
+        nc.scalar.copy(
+            v_d[:].rearrange("p (r s) t -> p r s t", r=PACK),
+            v_g[:].rearrange("p t (s r) -> p r s t", r=PACK),
+        )
+        v_words = v_d[:].rearrange("p j t -> p (j t)").bitcast(F32)
+        v_j = tile([P, PACK, P, PACK], BF16, "v_j")
+        for h in range(2):
+            vt_ps = bank("vt_ps%d" % h, "A%d" % h)
+            for r in range(PACK):
+                nc.tensor.transpose(
+                    vt_ps[:, r * P : (r + 1) * P], v_words[:, 2 * r * P + h : 2 * (r + 1) * P : 2], ident[:]
+                )
+            nc.scalar.copy(
+                v_j[:, 2 * h : 2 * h + 2, :, :],
+                vt_ps[:].bitcast(BF16).rearrange("p (r d e) -> p e d r", r=PACK, e=2),
+            )
+
+        def quantize(src, name, fmt):
+            codes = tile([P, N], U32, name + "_codes")
+            scales = tile([P, N], U8, name + "_scales")
+            nc.vector.quantize_mx(out=codes[:].bitcast(fmt), scales=scales[:], in_=src)
+            return codes, scales
+
+        u_d = tile([P, N, PACK], BF16, "u_d")
+        nc.vector.tensor_copy(u_d[:, :, 0], u_win[0][:].indirect(item_list[:]))
+        vd_codes, vd_scales = quantize(v_d[:].rearrange("p j t -> p (j t)"), "vd", E4M3)
+        nc.vector.tensor_copy(u_d[:, :, 1], u_win[1][:].indirect(item_list[:]))
+        vj_codes, vj_scales = quantize(v_j[:].rearrange("p t d r -> p (t d r)"), "vj", E4M3)
+        nc.vector.tensor_copy(u_d[:, :, 2], u_win[2][:].indirect(item_list[:]))
+        nc.vector.tensor_copy(u_d[:, :, 3], u_win[3][:].indirect(item_list[:]))
+        ud_codes, ud_scales = quantize(u_d[:].rearrange("p i t -> p (i t)"), "ud", E4M3)
+
+        a_ps = [bank("a_ps%d" % q, "A%d" % q) for q in range(PACK)]
+        for q in range(PACK):
+            cols = slice(q * P, (q + 1) * P)
+            nc.tensor.matmul_mx(
+                a_ps[q][:], lhsT=ud_codes[:, cols].bitcast(E4M3), lhsT_scale=ud_scales[:, cols],
+                rhs=vd_codes[:].bitcast(E4M3), rhs_scale=vd_scales[:], start=True, stop=True,
+            )
+
+        c_ps = [bank("c_ps%d" % r, "C%d" % r) for r in range(PACK)]
+        y_mean = []
+        for q in range(PACK):
+            neg_y = tile([P, PACK, P], F32, "neg_y%d" % q)
+            neg_sum = tile([P, 1], F32, "neg_sum%d" % q)
+            nc.scalar.activation(
+                neg_y[:], y_sb[q][:].rearrange("p (s r) -> p r s", r=PACK), ACT.Copy, scale=-1.0, accum_out=neg_sum[:]
+            )
+            y_mean.append(neg_sum)
+            for r in range(PACK):
+                nc.tensor.matmul(
+                    c_ps[r][:, q * P : (q + 1) * P], lhsT=neg_y[:, r, :], rhs=ident[:],
+                    start=(q == 0), stop=False, is_transpose=True,
+                )
+
+        for q in range(PACK):
+            b = tile([P, N], F32, "b%d" % q)
+            row_sum = tile([P, 1], F32, "row_sum%d" % q)
+            shift = tile([P, 1], F32, "shift%d" % q)
+            nc.vector.scalar_tensor_tensor(
+                b[:], a_ps[q][:], s_col[:, q : q + 1], t_row[:], ALU.mult, ALU.mult, accum_out=row_sum[:]
+            )
+            nc.gpsimd.tensor_scalar(shift[:], row_sum[:], y_mean[q][:], -1.0 / N, ALU.add, ALU.mult)
+            nc.scalar.activation(b[:], b[:], ACT.Identity, scale=1.0, bias=shift[:])
+            for r in range(PACK):
+                nc.tensor.matmul(
+                    c_ps[r][:, q * P : (q + 1) * P], lhsT=b[:, r * P : (r + 1) * P], rhs=ident[:],
+                    start=False, stop=(q == PACK - 1), is_transpose=True,
+                )
+
+        g_p = tile([P, PACK, N], BF16, "g_p", tag="v_g")
+        col_mean = [tile([P, 1], F32, "col_mean%d" % r) for r in range(PACK)]
+        for r in range(PACK):
+            junk = tile([P, N], BF16, "junk%d" % r)
+            if r == 1:
+                nc.vector.tensor_scalar(junk[:], c_ps[r][:], 1.0 / N, None, ALU.mult, ALU.add, accum_out=col_mean[r][:])
+            else:
+                nc.scalar.activation(junk[:], c_ps[r][:], ACT.Copy, scale=1.0 / N, accum_out=col_mean[r][:])
+        for r in range(PACK):
+            nc.vector.scalar_tensor_tensor(
+                g_p[:, r, :], c_ps[r][:], col_mean[r][:], w[r][:], ALU.subtract, ALU.mult
+            )
+        g_j = tile([P, N, PACK], BF16, "g_j", tag="v_d")
+        SPLIT = 352
+        nc.scalar.copy(g_j[:, SPLIT:N, :], g_p[:, :, SPLIT:N].rearrange("p r i -> p i r"))
+        nc.vector.tensor_copy(g_j[:, 0:SPLIT, :], g_p[:, :, 0:SPLIT].rearrange("p r i -> p i r"))
+        g_codes, g_scales = quantize(g_j[:].rearrange("p i r -> p (i r)"), "g", E5M2)
+
+        out_rows = out_0.rearrange("(p t) c -> p t c", t=PACK)
+        planes = [tile([P, PACK, CW], BF16, "planes%d" % c) for c in range(CHUNKS)]
+        for t in range(PACK):
+            cols = slice(t * P, (t + 1) * P)
+            du_ps = bank("du_ps%d" % t, "A%d" % t)
+            nc.tensor.matmul_mx(
+                du_ps[:], lhsT=vj_codes[:, cols].bitcast(E4M3), lhsT_scale=vj_scales[:, cols],
+                rhs=g_codes[:].bitcast(E5M2), rhs_scale=g_scales[:], start=True, stop=True,
+            )
+            du = tile([P, N], F32, "du%d" % t, tag="y_sb%d" % t)
+            nc.scalar.copy(du[:], du_ps[:])
+            nc.vector.tensor_copy(out_win[t][:].indirect(item_list[:]), du[:])
+            nc.sync.dma_start(out_rows[:, t, :], out_win[t][:])
+            if t < PACK - 1:
+                for c in range(CHUNKS):
+                    nc.scalar.copy(planes[c][:, t, :], out_win[t][:, c * CW : (c + 1) * CW])
+
+        last = PACK - 1
+        woven = [tile([P, CW, PACK], BF16, "woven%d" % c) for c in range(CHUNKS)]
+        out_codes = [tile([P, CW], U32, "out_codes%d" % c) for c in range(CHUNKS)]
+        out_scales = tile([P, T], U8, "out_scales")
+        words = out_1[0].rearrange("p c l -> p (c l)").bitcast(I32)
+
+        def cast(eng, c):
+            if eng == "act":
+                nc.scalar.copy(planes[c][:, last, :], out_win[last][:, c * CW : (c + 1) * CW])
+            else:
+                nc.vector.tensor_copy(planes[c][:, last, :], out_win[last][:, c * CW : (c + 1) * CW])
+
+        def weave(eng, c):
+            if eng == "act":
+                nc.scalar.copy(woven[c][:], planes[c][:].rearrange("p t c -> p c t"))
+            else:
+                nc.vector.tensor_copy(woven[c][:], planes[c][:].rearrange("p t c -> p c t"))
+
+        def emit(c):
+            cols = slice(c * CW, (c + 1) * CW)
+            nc.vector.quantize_mx(
+                out=out_codes[c][:].bitcast(E4M3), scales=out_scales[:, cols],
+                in_=woven[c][:].rearrange("p c t -> p (c t)"),
+            )
+            nc.sync.dma_start(words[:, cols], out_codes[c][:].bitcast(I32))
+
+        cast("act", 1)
+        cast("dve", 0)
+        cast("dve", 2)
+        cast("dve", 3)
+        weave("act", 1)
+        weave("dve", 0)
+        weave("act", 3)
+        weave("dve", 2)
+        emit(0)
+        emit(1)
+        emit(2)
+        emit(3)
+        scale_rows = out_2[0].bitcast(I32)
+        for Q in range(PACK):
+            eng = nc.sync if Q % 2 == 0 else nc.scalar
+            eng.dma_start(scale_rows[PACK * Q : PACK * (Q + 1), :], out_scales[32 * Q : 32 * Q + PACK, :].bitcast(I32))

@@ -39,8 +39,6 @@ def tile_attend_gcentre_pl_kernel(tc, uT, vT, su, sv, y, offs, qoffs, out_0, out
 
         item_list = held.tile([P, N // 16], U16, name="item_list")
         partner_list = held.tile([P, N // 16], U16, name="partner_list")
-        nc.sync.dma_start(partner_list[:], qoffs)
-        nc.sync.dma_start(item_list[:], offs)
 
         u_rows = uT.rearrange("(p t) c -> p t c", t=PACK)
         v_rows = vT.rearrange("(p t) c -> p t c", t=PACK)
@@ -52,9 +50,12 @@ def tile_attend_gcentre_pl_kernel(tc, uT, vT, su, sv, y, offs, qoffs, out_0, out
         RUN = T // P
         sv_run = tile([P, RUN], F32, "sv_run")
         su_run = tile([P, RUN], F32, "su_run")
-        nc.sync.dma_start(sv_run[:], sv[0].rearrange("(p k) -> p k", k=RUN))
-        nc.sync.dma_start(su_run[:], su[0].rearrange("(p k) -> p k", k=RUN))
-        for t in range(PACK):
+        nc.scalar.dma_start(sv_run[:], sv[0].rearrange("(p k) -> p k", k=RUN))
+        nc.scalar.dma_start(su_run[:], su[0].rearrange("(p k) -> p k", k=RUN))
+        nc.sync.dma_start(partner_list[:], qoffs)
+        nc.sync.dma_start(v_win[0][:], v_rows[:, 0, :])
+        nc.sync.dma_start(item_list[:], offs)
+        for t in range(1, PACK):
             nc.sync.dma_start(v_win[t][:], v_rows[:, t, :])
         for t in range(PACK):
             nc.sync.dma_start(u_win[t][:], u_rows[:, t, :])
@@ -65,7 +66,7 @@ def tile_attend_gcentre_pl_kernel(tc, uT, vT, su, sv, y, offs, qoffs, out_0, out
         make_identity(nc, ident[:])
         out_win = [tile([P, T], F32, "out_win%d" % t) for t in range(PACK)]
         for t in range(PACK):
-            nc.gpsimd.memset(out_win[t][:], 0.0)
+            nc.vector.memset(out_win[t][:], 0.0)
 
         for run, win, tagc in ((sv_run, sv_win, "A"), (su_run, su_win, "C")):
             for bk in range(PACK):
@@ -89,7 +90,7 @@ def tile_attend_gcentre_pl_kernel(tc, uT, vT, su, sv, y, offs, qoffs, out_0, out
                 nc.vector.tensor_copy(s_g[:], su_win[:].indirect(item_list[:]))
 
         t_row = tile([P, N], F32, "t_row")
-        nc.scalar.copy(t_row[:].rearrange("p (r s) -> p r s", r=PACK), t_g[:].rearrange("p (s r) -> p r s", r=PACK))
+        nc.scalar.copy(t_row[:].rearrange("p (r s) -> p s r", r=PACK), t_g[:].rearrange("p (s r) -> p s r", r=PACK))
         t_ps = bank("t_ps", "A2")
         s_ps = bank("s_ps", "A3")
         for r in range(PACK):
@@ -106,8 +107,8 @@ def tile_attend_gcentre_pl_kernel(tc, uT, vT, su, sv, y, offs, qoffs, out_0, out
 
         v_d = tile([P, N, PACK], BF16, "v_d")
         nc.scalar.copy(
-            v_d[:].rearrange("p (r s) t -> p r s t", r=PACK),
-            v_g[:].rearrange("p t (s r) -> p r s t", r=PACK),
+            v_d[:].rearrange("p (r s) t -> p s r t", r=PACK),
+            v_g[:].rearrange("p t (s r) -> p s r t", r=PACK),
         )
         v_words = v_d[:].rearrange("p j t -> p (j t)").bitcast(F32)
         v_j = tile([P, PACK, P, PACK], BF16, "v_j")
@@ -122,8 +123,8 @@ def tile_attend_gcentre_pl_kernel(tc, uT, vT, su, sv, y, offs, qoffs, out_0, out
                 vt_ps[:].bitcast(BF16).rearrange("p (r d e) -> p e d r", r=PACK, e=2),
             )
 
-        def quantize(src, name, fmt):
-            codes = tile([P, N], U32, name + "_codes")
+        def quantize(src, name, fmt, tag=None):
+            codes = tile([P, N], U32, name + "_codes", tag=tag)
             scales = tile([P, N], U8, name + "_scales")
             nc.vector.quantize_mx(out=codes[:].bitcast(fmt), scales=scales[:], in_=src)
             return codes, scales
@@ -132,54 +133,78 @@ def tile_attend_gcentre_pl_kernel(tc, uT, vT, su, sv, y, offs, qoffs, out_0, out
         nc.vector.tensor_copy(u_d[:, :, 0], u_win[0][:].indirect(item_list[:]))
         vd_codes, vd_scales = quantize(v_d[:].rearrange("p j t -> p (j t)"), "vd", E4M3)
         nc.vector.tensor_copy(u_d[:, :, 1], u_win[1][:].indirect(item_list[:]))
-        vj_codes, vj_scales = quantize(v_j[:].rearrange("p t d r -> p (t d r)"), "vj", E4M3)
         nc.vector.tensor_copy(u_d[:, :, 2], u_win[2][:].indirect(item_list[:]))
-        nc.vector.tensor_copy(u_d[:, :, 3], u_win[3][:].indirect(item_list[:]))
-        ud_codes, ud_scales = quantize(u_d[:].rearrange("p i t -> p (i t)"), "ud", E4M3)
+        H = N // 2
+        ud_codes = [tile([P, H], U32, "ud_codes%d" % h) for h in range(2)]
+        ud_scales = [tile([P, H], U8, "ud_scales%d" % h) for h in range(2)]
+        for h in range(2):
+            nc.vector.tensor_copy(
+                u_d[:, h * H : (h + 1) * H, 3], u_win[3][:].indirect(item_list[:, h * H // 16 : (h + 1) * H // 16])
+            )
+            nc.vector.quantize_mx(
+                out=ud_codes[h][:].bitcast(E4M3), scales=ud_scales[h][:],
+                in_=u_d[:, h * H : (h + 1) * H, :].rearrange("p i t -> p (i t)"),
+            )
 
         a_ps = [bank("a_ps%d" % q, "A%d" % q) for q in range(PACK)]
         for q in range(PACK):
-            cols = slice(q * P, (q + 1) * P)
+            cols = slice((q % 2) * P, (q % 2 + 1) * P)
             nc.tensor.matmul_mx(
-                a_ps[q][:], lhsT=ud_codes[:, cols].bitcast(E4M3), lhsT_scale=ud_scales[:, cols],
+                a_ps[q][:], lhsT=ud_codes[q // 2][:, cols].bitcast(E4M3), lhsT_scale=ud_scales[q // 2][:, cols],
                 rhs=vd_codes[:].bitcast(E4M3), rhs_scale=vd_scales[:], start=True, stop=True,
             )
 
         c_ps = [bank("c_ps%d" % r, "C%d" % r) for r in range(PACK)]
-        y_mean = []
+        EARLY = 2
+        neg_y, neg_sum = [], []
         for q in range(PACK):
-            neg_y = tile([P, PACK, P], F32, "neg_y%d" % q)
-            neg_sum = tile([P, 1], F32, "neg_sum%d" % q)
+            ny = tile([P, PACK, P], F32, "neg_y%d" % q)
+            ns = tile([P, 1], F32, "neg_sum%d" % q)
             nc.scalar.activation(
-                neg_y[:], y_sb[q][:].rearrange("p (s r) -> p r s", r=PACK), ACT.Copy, scale=-1.0, accum_out=neg_sum[:]
+                ny[:].rearrange("p r s -> p s r"), y_sb[q][:].rearrange("p (s r) -> p s r", r=PACK), ACT.Copy, scale=-1.0, accum_out=ns[:]
             )
-            y_mean.append(neg_sum)
-            for r in range(PACK):
-                nc.tensor.matmul(
-                    c_ps[r][:, q * P : (q + 1) * P], lhsT=neg_y[:, r, :], rhs=ident[:],
-                    start=(q == 0), stop=False, is_transpose=True,
-                )
+            neg_y.append(ny)
+            neg_sum.append(ns)
+            if q < EARLY:
+                for r in range(PACK):
+                    nc.tensor.matmul(
+                        c_ps[r][:, q * P : (q + 1) * P], lhsT=ny[:, r, :], rhs=ident[:],
+                        start=(q == 0), stop=False, is_transpose=True,
+                    )
+
+        b = [tile([P, N], F32, "b%d" % q) for q in range(PACK)]
+        row_sum = [tile([P, 1], F32, "row_sum%d" % q) for q in range(PACK)]
+        shift = [tile([P, 1], F32, "shift%d" % q) for q in range(PACK)]
+
+        def row_shift(q):
+            nc.vector.tensor_scalar(shift[q][:], row_sum[q][:], neg_sum[q][:], -1.0 / N, ALU.add, ALU.mult)
 
         for q in range(PACK):
-            b = tile([P, N], F32, "b%d" % q)
-            row_sum = tile([P, 1], F32, "row_sum%d" % q)
-            shift = tile([P, 1], F32, "shift%d" % q)
             nc.vector.scalar_tensor_tensor(
-                b[:], a_ps[q][:], s_col[:, q : q + 1], t_row[:], ALU.mult, ALU.mult, accum_out=row_sum[:]
+                b[q][:], a_ps[q][:], s_col[:, q : q + 1], t_row[:], ALU.mult, ALU.mult, accum_out=row_sum[q][:]
             )
-            nc.gpsimd.tensor_scalar(shift[:], row_sum[:], y_mean[q][:], -1.0 / N, ALU.add, ALU.mult)
-            nc.scalar.activation(b[:], b[:], ACT.Identity, scale=1.0, bias=shift[:])
+            if q > 0:
+                row_shift(q - 1)
+        row_shift(PACK - 1)
+        for q in range(PACK):
+            if q < EARLY:
+                nc.scalar.activation(b[q][:], b[q][:], ACT.Identity, scale=1.0, bias=shift[q][:])
+            else:
+                nc.vector.scalar_tensor_tensor(
+                    b[q][:], b[q][:], shift[q][:], neg_y[q][:].rearrange("p r s -> p (r s)"), ALU.add, ALU.add
+                )
             for r in range(PACK):
                 nc.tensor.matmul(
-                    c_ps[r][:, q * P : (q + 1) * P], lhsT=b[:, r * P : (r + 1) * P], rhs=ident[:],
+                    c_ps[r][:, q * P : (q + 1) * P], lhsT=b[q][:, r * P : (r + 1) * P], rhs=ident[:],
                     start=False, stop=(q == PACK - 1), is_transpose=True,
                 )
 
+        vj_codes, vj_scales = quantize(v_j[:].rearrange("p t d r -> p (t d r)"), "vj", E4M3, tag="neg_y3")
         g_p = tile([P, PACK, N], BF16, "g_p", tag="v_g")
         col_mean = [tile([P, 1], F32, "col_mean%d" % r) for r in range(PACK)]
         for r in range(PACK):
             junk = tile([P, N], BF16, "junk%d" % r)
-            if r == 1:
+            if r == 0:
                 nc.vector.tensor_scalar(junk[:], c_ps[r][:], 1.0 / N, None, ALU.mult, ALU.add, accum_out=col_mean[r][:])
             else:
                 nc.scalar.activation(junk[:], c_ps[r][:], ACT.Copy, scale=1.0 / N, accum_out=col_mean[r][:])
@@ -190,11 +215,20 @@ def tile_attend_gcentre_pl_kernel(tc, uT, vT, su, sv, y, offs, qoffs, out_0, out
         g_j = tile([P, N, PACK], BF16, "g_j", tag="v_d")
         SPLIT = 352
         nc.scalar.copy(g_j[:, SPLIT:N, :], g_p[:, :, SPLIT:N].rearrange("p r i -> p i r"))
-        nc.vector.tensor_copy(g_j[:, 0:SPLIT, :], g_p[:, :, 0:SPLIT].rearrange("p r i -> p i r"))
-        g_codes, g_scales = quantize(g_j[:].rearrange("p i r -> p (i r)"), "g", E5M2)
+        nc.vector.tensor_copy(g_j[:, 0:H, :], g_p[:, :, 0:H].rearrange("p r i -> p i r"))
+        nc.vector.tensor_copy(g_j[:, H:SPLIT, :], g_p[:, :, H:SPLIT].rearrange("p r i -> p i r"))
+        g_codes = tile([P, N], U32, "g_codes")
+        g_scales = tile([P, N], U8, "g_scales")
+        for h in range(2):
+            nc.vector.quantize_mx(
+                out=g_codes[:, h * H : (h + 1) * H].bitcast(E5M2), scales=g_scales[:, h * H : (h + 1) * H],
+                in_=g_j[:, h * H : (h + 1) * H, :].rearrange("p i r -> p (i r)"),
+            )
 
         out_rows = out_0.rearrange("(p t) c -> p t c", t=PACK)
-        planes = [tile([P, PACK, CW], BF16, "planes%d" % c) for c in range(CHUNKS)]
+        last = PACK - 1
+        woven = [tile([P, CW, PACK], BF16, "woven%d" % c) for c in range(CHUNKS)]
+        du = []
         for t in range(PACK):
             cols = slice(t * P, (t + 1) * P)
             du_ps = bank("du_ps%d" % t, "A%d" % t)
@@ -202,52 +236,42 @@ def tile_attend_gcentre_pl_kernel(tc, uT, vT, su, sv, y, offs, qoffs, out_0, out
                 du_ps[:], lhsT=vj_codes[:, cols].bitcast(E4M3), lhsT_scale=vj_scales[:, cols],
                 rhs=g_codes[:].bitcast(E5M2), rhs_scale=g_scales[:], start=True, stop=True,
             )
-            du = tile([P, N], F32, "du%d" % t, tag="y_sb%d" % t)
-            nc.scalar.copy(du[:], du_ps[:])
-            nc.vector.tensor_copy(out_win[t][:].indirect(item_list[:]), du[:])
-            nc.sync.dma_start(out_rows[:, t, :], out_win[t][:])
-            if t < PACK - 1:
-                for c in range(CHUNKS):
-                    nc.scalar.copy(planes[c][:, t, :], out_win[t][:, c * CW : (c + 1) * CW])
+            du.append(tile([P, N], F32, "du%d" % t, tag="y_sb%d" % t))
+            if t == 0:
+                for h in range(2):
+                    nc.scalar.copy(du[t][:, h * H : (h + 1) * H], du_ps[:, h * H : (h + 1) * H])
+            else:
+                nc.scalar.copy(du[t][:], du_ps[:])
+        for t in range(PACK):
+            if t == 0:
+                for h in range(2):
+                    nc.vector.tensor_copy(
+                        out_win[t][:].indirect(item_list[:, h * H // 16 : (h + 1) * H // 16]), du[t][:, h * H : (h + 1) * H]
+                    )
+            else:
+                nc.vector.tensor_copy(out_win[t][:].indirect(item_list[:]), du[t][:])
+            (nc.sync if t < last else nc.scalar).dma_start(out_rows[:, t, :], out_win[t][:])
+            for c in range(CHUNKS):
+                src = out_win[t][:, c * CW : (c + 1) * CW]
+                if c % 2 == 1:
+                    nc.scalar.copy(woven[c][:, :, t], src)
+                elif t < last - 1:
+                    nc.gpsimd.tensor_copy(woven[c][:, :, t], src)
+                elif t < last:
+                    nc.gpsimd.tensor_copy(woven[c][:, :, t : t + 2], src.unsqueeze(2).to_broadcast([P, CW, 2]))
+                else:
+                    nc.vector.tensor_copy(woven[c][:, :, t], src)
 
-        last = PACK - 1
-        woven = [tile([P, CW, PACK], BF16, "woven%d" % c) for c in range(CHUNKS)]
         out_codes = [tile([P, CW], U32, "out_codes%d" % c) for c in range(CHUNKS)]
         out_scales = tile([P, T], U8, "out_scales")
         words = out_1[0].rearrange("p c l -> p (c l)").bitcast(I32)
-
-        def cast(eng, c):
-            if eng == "act":
-                nc.scalar.copy(planes[c][:, last, :], out_win[last][:, c * CW : (c + 1) * CW])
-            else:
-                nc.vector.tensor_copy(planes[c][:, last, :], out_win[last][:, c * CW : (c + 1) * CW])
-
-        def weave(eng, c):
-            if eng == "act":
-                nc.scalar.copy(woven[c][:], planes[c][:].rearrange("p t c -> p c t"))
-            else:
-                nc.vector.tensor_copy(woven[c][:], planes[c][:].rearrange("p t c -> p c t"))
-
-        def emit(c):
+        for c in (0, 2, 1, 3):
             cols = slice(c * CW, (c + 1) * CW)
             nc.vector.quantize_mx(
                 out=out_codes[c][:].bitcast(E4M3), scales=out_scales[:, cols],
                 in_=woven[c][:].rearrange("p c t -> p (c t)"),
             )
             nc.sync.dma_start(words[:, cols], out_codes[c][:].bitcast(I32))
-
-        cast("act", 1)
-        cast("dve", 0)
-        cast("dve", 2)
-        cast("dve", 3)
-        weave("act", 1)
-        weave("dve", 0)
-        weave("act", 3)
-        weave("dve", 2)
-        emit(0)
-        emit(1)
-        emit(2)
-        emit(3)
         scale_rows = out_2[0].bitcast(I32)
         for Q in range(PACK):
             eng = nc.sync if Q % 2 == 0 else nc.scalar

@@ -18,8 +18,8 @@ P = 128
 PACK = 4
 N = 512
 T = 2048
-CHUNKS = 4
-CW = T // CHUNKS
+CHUNK_COLS = ((0, 512), (512, 1024), (1024, 1536), (1536, 1792), (1792, 2048))
+SCALAR_FROM = 1024
 
 FLOPS = 2 * 2 * 512 * 512 * 512
 
@@ -64,9 +64,6 @@ def tile_attend_gcentre_pl_kernel(tc, uT, vT, su, sv, y, offs, qoffs, out_0, out
 
         ident = tile([P, P], F32, "ident")
         make_identity(nc, ident[:])
-        out_win = [tile([P, T], F32, "out_win%d" % t) for t in range(PACK)]
-        for t in range(PACK):
-            nc.vector.memset(out_win[t][:], 0.0)
 
         for run, win, tagc in ((sv_run, sv_win, "A"), (su_run, su_win, "C")):
             for bk in range(PACK):
@@ -79,6 +76,11 @@ def tile_attend_gcentre_pl_kernel(tc, uT, vT, su, sv, y, offs, qoffs, out_0, out
                     sp[:].rearrange("m (k p) -> m p k", k=PACK),
                 )
 
+        g_codes = tile([P, N], U32, "g_codes")
+        g_scales = tile([P, N], U8, "g_scales")
+        nc.vector.memset(g_codes[:, N // 2 : N], 0)
+        nc.vector.memset(g_scales[:, N // 2 : N], 0)
+
         v_g = tile([P, PACK, N], BF16, "v_g")
         s_g = tile([P, N], F32, "s_g")
         t_g = tile([P, N], F32, "t_g")
@@ -88,6 +90,10 @@ def tile_attend_gcentre_pl_kernel(tc, uT, vT, su, sv, y, offs, qoffs, out_0, out
                 nc.vector.tensor_copy(t_g[:], sv_win[:].indirect(partner_list[:]))
             if t == 2:
                 nc.vector.tensor_copy(s_g[:], su_win[:].indirect(item_list[:]))
+
+        out_win = [tile([P, T], F32, "out_win%d" % t, tag="v_win%d" % t) for t in range(PACK)]
+        for t in range(PACK):
+            nc.gpsimd.memset(out_win[t][:], 0.0)
 
         t_row = tile([P, N], F32, "t_row")
         nc.scalar.copy(t_row[:].rearrange("p (r s) -> p s r", r=PACK), t_g[:].rearrange("p (s r) -> p s r", r=PACK))
@@ -155,7 +161,7 @@ def tile_attend_gcentre_pl_kernel(tc, uT, vT, su, sv, y, offs, qoffs, out_0, out
             )
 
         c_ps = [bank("c_ps%d" % r, "C%d" % r) for r in range(PACK)]
-        EARLY = 2
+        EARLY = 3
         neg_y, neg_sum = [], []
         for q in range(PACK):
             ny = tile([P, PACK, P], F32, "neg_y%d" % q)
@@ -190,9 +196,12 @@ def tile_attend_gcentre_pl_kernel(tc, uT, vT, su, sv, y, offs, qoffs, out_0, out
             if q < EARLY:
                 nc.scalar.activation(b[q][:], b[q][:], ACT.Identity, scale=1.0, bias=shift[q][:])
             else:
-                nc.vector.scalar_tensor_tensor(
-                    b[q][:], b[q][:], shift[q][:], neg_y[q][:].rearrange("p r s -> p (r s)"), ALU.add, ALU.add
-                )
+                for h in range(2):
+                    half = slice(h * H, (h + 1) * H)
+                    nc.vector.scalar_tensor_tensor(
+                        b[q][:, half], b[q][:, half], shift[q][:],
+                        neg_y[q][:].rearrange("p r s -> p (r s)")[:, half], ALU.add, ALU.add,
+                    )
             for r in range(PACK):
                 nc.tensor.matmul(
                     c_ps[r][:, q * P : (q + 1) * P], lhsT=b[q][:, r * P : (r + 1) * P], rhs=ident[:],
@@ -204,44 +213,41 @@ def tile_attend_gcentre_pl_kernel(tc, uT, vT, su, sv, y, offs, qoffs, out_0, out
         col_mean = [tile([P, 1], F32, "col_mean%d" % r) for r in range(PACK)]
         for r in range(PACK):
             junk = tile([P, N], BF16, "junk%d" % r)
-            if r == 0:
+            if r == 1:
                 nc.vector.tensor_scalar(junk[:], c_ps[r][:], 1.0 / N, None, ALU.mult, ALU.add, accum_out=col_mean[r][:])
             else:
                 nc.scalar.activation(junk[:], c_ps[r][:], ACT.Copy, scale=1.0 / N, accum_out=col_mean[r][:])
-        for r in range(PACK):
-            nc.vector.scalar_tensor_tensor(
-                g_p[:, r, :], c_ps[r][:], col_mean[r][:], w[r][:], ALU.subtract, ALU.mult
-            )
         g_j = tile([P, N, PACK], BF16, "g_j", tag="v_d")
-        SPLIT = 352
-        nc.scalar.copy(g_j[:, SPLIT:N, :], g_p[:, :, SPLIT:N].rearrange("p r i -> p i r"))
-        nc.vector.tensor_copy(g_j[:, 0:H, :], g_p[:, :, 0:H].rearrange("p r i -> p i r"))
-        nc.vector.tensor_copy(g_j[:, H:SPLIT, :], g_p[:, :, H:SPLIT].rearrange("p r i -> p i r"))
-        g_codes = tile([P, N], U32, "g_codes")
-        g_scales = tile([P, N], U8, "g_scales")
-        for h in range(2):
-            nc.vector.quantize_mx(
-                out=g_codes[:, h * H : (h + 1) * H].bitcast(E5M2), scales=g_scales[:, h * H : (h + 1) * H],
-                in_=g_j[:, h * H : (h + 1) * H, :].rearrange("p i r -> p (i r)"),
-            )
-
         out_rows = out_0.rearrange("(p t) c -> p t c", t=PACK)
         last = PACK - 1
-        woven = [tile([P, CW, PACK], BF16, "woven%d" % c) for c in range(CHUNKS)]
-        du = []
-        for t in range(PACK):
-            cols = slice(t * P, (t + 1) * P)
-            du_ps = bank("du_ps%d" % t, "A%d" % t)
+        woven = [tile([P, hi - lo, PACK], BF16, "woven%d" % lo) for lo, hi in CHUNK_COLS]
+        du = [tile([P, N], F32, "du%d" % t, tag="y_sb%d" % t) for t in range(PACK)]
+
+        def second_product(t, bank_tag, cols):
+            du_ps = bank("du_ps%d_%d" % (t, cols.start), bank_tag)
+            rows = slice(t * P, (t + 1) * P)
             nc.tensor.matmul_mx(
-                du_ps[:], lhsT=vj_codes[:, cols].bitcast(E4M3), lhsT_scale=vj_scales[:, cols],
+                du_ps[:], lhsT=vj_codes[:, rows].bitcast(E4M3), lhsT_scale=vj_scales[:, rows],
                 rhs=g_codes[:].bitcast(E5M2), rhs_scale=g_scales[:], start=True, stop=True,
             )
-            du.append(tile([P, N], F32, "du%d" % t, tag="y_sb%d" % t))
-            if t == 0:
-                for h in range(2):
-                    nc.scalar.copy(du[t][:, h * H : (h + 1) * H], du_ps[:, h * H : (h + 1) * H])
-            else:
-                nc.scalar.copy(du[t][:], du_ps[:])
+            nc.scalar.copy(du[t][:, cols], du_ps[:, cols])
+
+        SHARE = 176
+        for h in range(2):
+            lo, hi = h * H, (h + 1) * H
+            for r in range(PACK):
+                nc.vector.scalar_tensor_tensor(
+                    g_p[:, r, lo:hi], c_ps[r][:, lo:hi], col_mean[r][:], w[r][:, lo:hi], ALU.subtract, ALU.mult
+                )
+            nc.scalar.copy(g_j[:, lo + SHARE : hi, :], g_p[:, :, lo + SHARE : hi].rearrange("p r i -> p i r"))
+            nc.vector.tensor_copy(g_j[:, lo : lo + SHARE, :], g_p[:, :, lo : lo + SHARE].rearrange("p r i -> p i r"))
+            nc.vector.quantize_mx(
+                out=g_codes[:, lo:hi].bitcast(E5M2), scales=g_scales[:, lo:hi],
+                in_=g_j[:, lo:hi, :].rearrange("p i r -> p (i r)"),
+            )
+            second_product(0, "A%d" % h, slice(lo, hi))
+        for t in range(1, PACK):
+            second_product(t, "A%d" % ((t + 1) % PACK), slice(0, N))
         for t in range(PACK):
             if t == 0:
                 for h in range(2):
@@ -251,22 +257,22 @@ def tile_attend_gcentre_pl_kernel(tc, uT, vT, su, sv, y, offs, qoffs, out_0, out
             else:
                 nc.vector.tensor_copy(out_win[t][:].indirect(item_list[:]), du[t][:])
             (nc.sync if t < last else nc.scalar).dma_start(out_rows[:, t, :], out_win[t][:])
-            for c in range(CHUNKS):
-                src = out_win[t][:, c * CW : (c + 1) * CW]
-                if c % 2 == 1:
+            for c, (lo, hi) in enumerate(CHUNK_COLS):
+                src = out_win[t][:, lo:hi]
+                if lo >= SCALAR_FROM:
                     nc.scalar.copy(woven[c][:, :, t], src)
                 elif t < last - 1:
                     nc.gpsimd.tensor_copy(woven[c][:, :, t], src)
                 elif t < last:
-                    nc.gpsimd.tensor_copy(woven[c][:, :, t : t + 2], src.unsqueeze(2).to_broadcast([P, CW, 2]))
+                    nc.gpsimd.tensor_copy(woven[c][:, :, t : t + 2], src.unsqueeze(2).to_broadcast([P, hi - lo, 2]))
                 else:
                     nc.vector.tensor_copy(woven[c][:, :, t], src)
 
-        out_codes = [tile([P, CW], U32, "out_codes%d" % c) for c in range(CHUNKS)]
+        out_codes = [tile([P, hi - lo], U32, "out_codes%d" % lo) for lo, hi in CHUNK_COLS]
         out_scales = tile([P, T], U8, "out_scales")
         words = out_1[0].rearrange("p c l -> p (c l)").bitcast(I32)
-        for c in (0, 2, 1, 3):
-            cols = slice(c * CW, (c + 1) * CW)
+        for c, (lo, hi) in enumerate(CHUNK_COLS):
+            cols = slice(lo, hi)
             nc.vector.quantize_mx(
                 out=out_codes[c][:].bitcast(E4M3), scales=out_scales[:, cols],
                 in_=woven[c][:].rearrange("p c t -> p (c t)"),

@@ -18,8 +18,9 @@ P = 128
 PACK = 4
 N = 512
 T = 2048
-CHUNK_COLS = ((0, 512), (512, 1024), (1024, 1536), (1536, 1792), (1792, 2048))
-SCALAR_FROM = 1024
+CHUNK_COLS = ((0, 512), (512, 768), (768, 1280), (1280, 1536), (1536, 1792), (1792, 2048))
+SCALAR_CHUNKS = (2, 3, 4)
+STORE_COLS = ((0, 768), (768, 1280), (1280, 1792), (1792, 2048))
 
 FLOPS = 2 * 2 * 512 * 512 * 512
 
@@ -259,25 +260,32 @@ def tile_attend_gcentre_pl_kernel(tc, uT, vT, su, sv, y, offs, qoffs, out_0, out
             (nc.sync if t < last else nc.scalar).dma_start(out_rows[:, t, :], out_win[t][:])
             for c, (lo, hi) in enumerate(CHUNK_COLS):
                 src = out_win[t][:, lo:hi]
-                if lo >= SCALAR_FROM:
+                if c in SCALAR_CHUNKS:
                     nc.scalar.copy(woven[c][:, :, t], src)
                 elif t < last - 1:
-                    nc.gpsimd.tensor_copy(woven[c][:, :, t], src)
+                    nc.gpsimd.tensor_scalar(woven[c][:, :, t], src, 1.0, 0.0, ALU.mult, ALU.add)
                 elif t < last:
-                    nc.gpsimd.tensor_copy(woven[c][:, :, t : t + 2], src.unsqueeze(2).to_broadcast([P, hi - lo, 2]))
-                else:
+                    nc.gpsimd.tensor_scalar(
+                        woven[c][:, :, t : t + 2], src.unsqueeze(2).to_broadcast([P, hi - lo, 2]), 1.0, 0.0, ALU.mult, ALU.add
+                    )
+                elif hi < T:
                     nc.vector.tensor_copy(woven[c][:, :, t], src)
+                else:
+                    nc.vector.tensor_copy(woven[c][:, 0:P, t], src[:, 0:P])
+                    nc.scalar.copy(woven[c][:, P:, t], src[:, P:])
 
-        out_codes = [tile([P, hi - lo], U32, "out_codes%d" % lo) for lo, hi in CHUNK_COLS]
+        out_codes = tile([P, T], U32, "out_codes")
         out_scales = tile([P, T], U8, "out_scales")
         words = out_1[0].rearrange("p c l -> p (c l)").bitcast(I32)
         for c, (lo, hi) in enumerate(CHUNK_COLS):
             cols = slice(lo, hi)
             nc.vector.quantize_mx(
-                out=out_codes[c][:].bitcast(E4M3), scales=out_scales[:, cols],
+                out=out_codes[:, cols].bitcast(E4M3), scales=out_scales[:, cols],
                 in_=woven[c][:].rearrange("p c t -> p (c t)"),
             )
-            nc.sync.dma_start(words[:, cols], out_codes[c][:].bitcast(I32))
+            for first, end in STORE_COLS:
+                if end == hi:
+                    nc.sync.dma_start(words[:, first:end], out_codes[:, first:end].bitcast(I32))
         scale_rows = out_2[0].bitcast(I32)
         for Q in range(PACK):
             eng = nc.sync if Q % 2 == 0 else nc.scalar

@@ -51,8 +51,8 @@ def tile_attend_gcentre_pl_kernel(tc, uT, vT, su, sv, y, offs, qoffs, out_0, out
         RUN = T // P
         sv_run = tile([P, RUN], F32, "sv_run")
         su_run = tile([P, RUN], F32, "su_run")
-        nc.scalar.dma_start(sv_run[:], sv[0].rearrange("(p k) -> p k", k=RUN))
-        nc.scalar.dma_start(su_run[:], su[0].rearrange("(p k) -> p k", k=RUN))
+        nc.sync.dma_start(sv_run[:], sv[0].rearrange("(p k) -> p k", k=RUN))
+        nc.sync.dma_start(su_run[:], su[0].rearrange("(p k) -> p k", k=RUN))
         nc.sync.dma_start(partner_list[:], qoffs)
         nc.sync.dma_start(v_win[0][:], v_rows[:, 0, :])
         nc.sync.dma_start(item_list[:], offs)
@@ -106,11 +106,8 @@ def tile_attend_gcentre_pl_kernel(tc, uT, vT, su, sv, y, offs, qoffs, out_0, out
             nc.tensor.transpose(s_ps[:, q * P : (q + 1) * P], s_g[:, q * P : (q + 1) * P], ident[:])
         t_col = tile([P, PACK], F32, "t_col")
         s_col = tile([P, PACK], F32, "s_col")
-        nc.scalar.copy(t_col[:], t_ps[:, 0:N:P])
-        nc.scalar.copy(s_col[:], s_ps[:, 0:N:P])
-        w = [tile([P, N], F32, "w%d" % r) for r in range(PACK)]
-        for r in range(PACK):
-            nc.scalar.activation(w[r][:], s_g[:], ACT.Copy, scale=t_col[:, r : r + 1])
+        nc.scalar.activation(t_col[:], t_ps[:, 0:N:P], ACT.Copy, scale=-1.0)
+        nc.scalar.activation(s_col[:], s_ps[:, 0:N:P], ACT.Copy, scale=-1.0)
 
         v_d = tile([P, N, PACK], BF16, "v_d")
         nc.scalar.copy(
@@ -129,6 +126,10 @@ def tile_attend_gcentre_pl_kernel(tc, uT, vT, su, sv, y, offs, qoffs, out_0, out
                 v_j[:, 2 * h : 2 * h + 2, :, :],
                 vt_ps[:].bitcast(BF16).rearrange("p (r d e) -> p e d r", r=PACK, e=2),
             )
+
+        w = [tile([P, N], F32, "w%d" % r) for r in range(PACK)]
+        for r in range(PACK):
+            nc.scalar.activation(w[r][:], s_g[:], ACT.Copy, scale=t_col[:, r : r + 1])
 
         def quantize(src, name, fmt, tag=None):
             codes = tile([P, N], U32, name + "_codes", tag=tag)
@@ -168,14 +169,14 @@ def tile_attend_gcentre_pl_kernel(tc, uT, vT, su, sv, y, offs, qoffs, out_0, out
             ny = tile([P, PACK, P], F32, "neg_y%d" % q)
             ns = tile([P, 1], F32, "neg_sum%d" % q)
             nc.scalar.activation(
-                ny[:].rearrange("p r s -> p s r"), y_sb[q][:].rearrange("p (s r) -> p s r", r=PACK), ACT.Copy, scale=-1.0, accum_out=ns[:]
+                ny[:].rearrange("p r s -> p s r"), y_sb[q][:].rearrange("p (s r) -> p s r", r=PACK), ACT.Copy, accum_out=ns[:]
             )
             neg_y.append(ny)
             neg_sum.append(ns)
             if q < EARLY:
                 for r in range(PACK):
                     nc.tensor.matmul(
-                        c_ps[r][:, q * P : (q + 1) * P], lhsT=ny[:, r, :], rhs=ident[:],
+                        c_ps[r][:, q * P : (q + 1) * P], lhsT=y_sb[q][:, r:N:PACK] if q == 0 else ny[:, r, :], rhs=ident[:],
                         start=(q == 0), stop=False, is_transpose=True,
                     )
 
@@ -203,11 +204,12 @@ def tile_attend_gcentre_pl_kernel(tc, uT, vT, su, sv, y, offs, qoffs, out_0, out
                         b[q][:, half], b[q][:, half], shift[q][:],
                         neg_y[q][:].rearrange("p r s -> p (r s)")[:, half], ALU.add, ALU.add,
                     )
-            for r in range(PACK):
-                nc.tensor.matmul(
-                    c_ps[r][:, q * P : (q + 1) * P], lhsT=b[q][:, r * P : (r + 1) * P], rhs=ident[:],
-                    start=False, stop=(q == PACK - 1), is_transpose=True,
-                )
+        turns = [(q, r) for q in range(2) for r in range(PACK)] + [(q, r) for r in range(PACK) for q in (2, 3)]
+        for q, r in turns:
+            nc.tensor.matmul(
+                c_ps[r][:, q * P : (q + 1) * P], lhsT=b[q][:, r * P : (r + 1) * P], rhs=ident[:],
+                start=False, stop=(q == PACK - 1), is_transpose=True,
+            )
 
         vj_codes, vj_scales = quantize(v_j[:].rearrange("p t d r -> p (t d r)"), "vj", E4M3, tag="neg_y3")
         g_p = tile([P, PACK, N], BF16, "g_p", tag="v_g")
@@ -233,8 +235,7 @@ def tile_attend_gcentre_pl_kernel(tc, uT, vT, su, sv, y, offs, qoffs, out_0, out
             )
             nc.scalar.copy(du[t][:, cols], du_ps[:, cols])
 
-        SHARE = 176
-        for h in range(2):
+        for h, SHARE in enumerate((144, 208)):
             lo, hi = h * H, (h + 1) * H
             for r in range(PACK):
                 nc.vector.scalar_tensor_tensor(

@@ -127,9 +127,6 @@ def tile_attend_gcentre_pl_kernel(tc, uT, vT, su, sv, y, offs, qoffs, out_0, out
                 vt_ps[:].bitcast(BF16).rearrange("p (r d e) -> p e d r", r=PACK, e=2),
             )
 
-        w = [tile([P, N], F32, "w%d" % r) for r in range(PACK)]
-        for r in range(PACK):
-            nc.scalar.activation(w[r][:], s_g[:], ACT.Copy, scale=t_col[:, r : r + 1])
 
         def quantize(src, name, fmt, tag=None):
             codes = tile([P, N], U32, name + "_codes", tag=tag)
@@ -153,6 +150,11 @@ def tile_attend_gcentre_pl_kernel(tc, uT, vT, su, sv, y, offs, qoffs, out_0, out
                 out=ud_codes[h][:].bitcast(E4M3), scales=ud_scales[h][:],
                 in_=u_d[:, h * H : (h + 1) * H, :].rearrange("p i t -> p (i t)"),
             )
+
+        w_all = tile([P, PACK, N], F32, "w_all", tag="u_d")
+        w = [w_all[:, r, :] for r in range(PACK)]
+        for r in range(PACK):
+            nc.gpsimd.tensor_scalar(w[r], s_g[:], t_col[:, r : r + 1], 0.0, ALU.mult, ALU.add)
 
         a_ps = [bank("a_ps%d" % q, "A%d" % q) for q in range(PACK)]
         for q in range(PACK):

@@ -18,9 +18,11 @@ P = 128
 PACK = 4
 N = 512
 T = 2048
-CHUNK_COLS = ((0, 512), (512, 768), (768, 1280), (1280, 1536), (1536, 1792), (1792, 2048))
-SCALAR_CHUNKS = (2, 3, 4)
-STORE_COLS = ((0, 768), (768, 1280), (1280, 1792), (1792, 2048))
+CHUNK_COLS = ((0, 1024), (1024, 2048))
+QUANT_COLS = ((0, 512), (512, 1024), (1024, 1536), (1536, 1792), (1792, 2048))
+SCALAR_CHUNKS = (1,)
+LAST_ON_VECTOR = 960
+STORE_COLS = ((0, 512), (512, 1024), (1024, 1536), (1536, 1792), (1792, 2048))
 
 FLOPS = 2 * 2 * 512 * 512 * 512
 
@@ -263,33 +265,38 @@ def tile_attend_gcentre_pl_kernel(tc, uT, vT, su, sv, y, offs, qoffs, out_0, out
             (nc.sync if t < last else nc.scalar).dma_start(out_rows[:, t, :], out_win[t][:])
             for c, (lo, hi) in enumerate(CHUNK_COLS):
                 src = out_win[t][:, lo:hi]
-                if c in SCALAR_CHUNKS:
+                if c in SCALAR_CHUNKS and t < last:
                     nc.scalar.copy(woven[c][:, :, t], src)
+                elif c in SCALAR_CHUNKS:
+                    for first, end in QUANT_COLS[2:]:
+                        nc.scalar.copy(woven[c][:, first - lo : end - lo, t], src[:, first - lo : end - lo])
                 elif t < last - 1:
                     nc.gpsimd.tensor_scalar(woven[c][:, :, t], src, 1.0, 0.0, ALU.mult, ALU.add)
                 elif t < last:
                     nc.gpsimd.tensor_scalar(
                         woven[c][:, :, t : t + 2], src.unsqueeze(2).to_broadcast([P, hi - lo, 2]), 1.0, 0.0, ALU.mult, ALU.add
                     )
-                elif hi < T:
-                    nc.vector.tensor_copy(woven[c][:, :, t], src)
                 else:
-                    nc.vector.tensor_copy(woven[c][:, 0:P, t], src[:, 0:P])
-                    nc.scalar.copy(woven[c][:, P:, t], src[:, P:])
+                    cut = LAST_ON_VECTOR
+                    nc.vector.tensor_copy(woven[c][:, 0:N, t], src[:, 0:N])
+                    nc.vector.tensor_copy(woven[c][:, N:cut, t], src[:, N:cut])
+                    nc.scalar.copy(woven[c][:, cut:, t], src[:, cut:])
 
         out_codes = tile([P, T], U32, "out_codes")
-        out_scales = tile([P, T], U8, "out_scales")
+        out_scales = tile([P, T // 2], U8, "out_scales")
         words = out_1[0].rearrange("p c l -> p (c l)").bitcast(I32)
-        for c, (lo, hi) in enumerate(CHUNK_COLS):
+        for lo, hi in QUANT_COLS:
+            c = [k for k, (first, end) in enumerate(CHUNK_COLS) if first <= lo < end][0]
+            base = CHUNK_COLS[c][0]
             cols = slice(lo, hi)
             nc.vector.quantize_mx(
-                out=out_codes[:, cols].bitcast(E4M3), scales=out_scales[:, cols],
-                in_=woven[c][:].rearrange("p c t -> p (c t)"),
+                out=out_codes[:, cols].bitcast(E4M3), scales=out_scales[PACK * (lo // (T // 2)) : P, lo % (T // 2) : lo % (T // 2) + hi - lo],
+                in_=woven[c][:, lo - base : hi - base, :].rearrange("p c t -> p (c t)"),
             )
             for first, end in STORE_COLS:
                 if end == hi:
                     nc.sync.dma_start(words[:, first:end], out_codes[:, first:end].bitcast(I32))
-        scale_rows = out_2[0].bitcast(I32)
+        scale_rows = out_2[0].bitcast(I32).rearrange("(q r) (a c) -> q a r c", r=PACK, a=2)
         for Q in range(PACK):
             eng = nc.sync if Q % 2 == 0 else nc.scalar
-            eng.dma_start(scale_rows[PACK * Q : PACK * (Q + 1), :], out_scales[32 * Q : 32 * Q + PACK, :].bitcast(I32))
+            eng.dma_start(scale_rows[Q], out_scales[32 * Q : 32 * Q + 2 * PACK, :].bitcast(I32))

@@ -166,7 +166,14 @@ def tile_attend_gcentre_pl_kernel(tc, uT, vT, su, sv, y, offs, qoffs, out_0, out
                 rhs=vd_codes[:].bitcast(E4M3), rhs_scale=vd_scales[:], start=True, stop=True,
             )
 
-        c_ps = [bank("c_ps%d" % r, "C%d" % r) for r in range(PACK)]
+        c_ps = [[bank("c_ps%d%d" % (h, k), "C%d" % (2 * h + k)) for k in range(2)] for h in range(2)]
+
+        def c_half(h, r):
+            return c_ps[h][r // 2][:, (r % 2) * H : (r % 2 + 1) * H]
+
+        def c_block(q, r):
+            return c_half(q // 2, r)[:, (q % 2) * P : (q % 2 + 1) * P]
+
         EARLY = 3
         neg_y, neg_sum = [], []
         for q in range(PACK):
@@ -180,8 +187,8 @@ def tile_attend_gcentre_pl_kernel(tc, uT, vT, su, sv, y, offs, qoffs, out_0, out
             if q < EARLY:
                 for r in range(PACK):
                     nc.tensor.matmul(
-                        c_ps[r][:, q * P : (q + 1) * P], lhsT=y_sb[q][:, r:N:PACK] if q == 0 else ny[:, r, :], rhs=ident[:],
-                        start=(q == 0), stop=False, is_transpose=True,
+                        c_block(q, r), lhsT=y_sb[q][:, r:N:PACK] if q == 0 else ny[:, r, :], rhs=ident[:],
+                        start=(q % 2 == 0 and r % 2 == 0), stop=False, is_transpose=True,
                     )
 
         b = [tile([P, N], F32, "b%d" % q) for q in range(PACK)]
@@ -208,22 +215,31 @@ def tile_attend_gcentre_pl_kernel(tc, uT, vT, su, sv, y, offs, qoffs, out_0, out
                         b[q][:, half], b[q][:, half], shift[q][:],
                         neg_y[q][:].rearrange("p r s -> p (r s)")[:, half], ALU.add, ALU.add,
                     )
-        turns = [(q, r) for q in range(2) for r in range(PACK)] + [(q, r) for r in range(PACK) for q in (2, 3)]
+        turns = [(q, r) for q in range(PACK) for r in range(PACK)]
         for q, r in turns:
             nc.tensor.matmul(
-                c_ps[r][:, q * P : (q + 1) * P], lhsT=b[q][:, r * P : (r + 1) * P], rhs=ident[:],
-                start=False, stop=(q == PACK - 1), is_transpose=True,
+                c_block(q, r), lhsT=b[q][:, r * P : (r + 1) * P], rhs=ident[:],
+                start=False, stop=(q % 2 == 1 and r % 2 == 1), is_transpose=True,
             )
 
         vj_codes, vj_scales = quantize(v_j[:].rearrange("p t d r -> p (t d r)"), "vj", E4M3, tag="neg_y3")
         g_p = tile([P, PACK, N], BF16, "g_p", tag="v_g")
         col_mean = [tile([P, 1], F32, "col_mean%d" % r) for r in range(PACK)]
+        part = [tile([P, 1], F32, "part%d" % r) for r in range(PACK)]
+        junk = [tile([P, N], BF16, "junk%d" % r) for r in range(PACK)]
         for r in range(PACK):
-            junk = tile([P, N], BF16, "junk%d" % r)
-            if r == 1:
-                nc.vector.tensor_scalar(junk[:], c_ps[r][:], 1.0 / N, None, ALU.mult, ALU.add, accum_out=col_mean[r][:])
+            nc.scalar.activation(
+                junk[r][:, 0:H], c_half(0, r), ACT.Copy, scale=1.0 / N if r < 2 else 1.0 / (N * H), accum_out=part[r][:]
+            )
+        for r in range(PACK):
+            if r < 2:
+                nc.vector.tensor_scalar(
+                    junk[r][:, H:N], c_half(1, r), 1.0 / N, part[r][:], ALU.mult, ALU.add, accum_out=col_mean[r][:]
+                )
             else:
-                nc.scalar.activation(junk[:], c_ps[r][:], ACT.Copy, scale=1.0 / N, accum_out=col_mean[r][:])
+                nc.scalar.activation(
+                    junk[r][:, H:N], c_half(1, r), ACT.Identity, scale=1.0 / N, bias=part[r][:], accum_out=col_mean[r][:]
+                )
         g_j = tile([P, N, PACK], BF16, "g_j", tag="v_d")
         out_rows = out_0.rearrange("(p t) c -> p t c", t=PACK)
         last = PACK - 1
@@ -243,7 +259,7 @@ def tile_attend_gcentre_pl_kernel(tc, uT, vT, su, sv, y, offs, qoffs, out_0, out
             lo, hi = h * H, (h + 1) * H
             for r in range(PACK):
                 nc.vector.scalar_tensor_tensor(
-                    g_p[:, r, lo:hi], c_ps[r][:, lo:hi], col_mean[r][:], w[r][:, lo:hi], ALU.subtract, ALU.mult
+                    g_p[:, r, lo:hi], c_half(h, r), col_mean[r][:], w[r][:, lo:hi], ALU.subtract, ALU.mult
                 )
             nc.scalar.copy(g_j[:, lo + SHARE : hi, :], g_p[:, :, lo + SHARE : hi].rearrange("p r i -> p i r"))
             nc.vector.tensor_copy(g_j[:, lo : lo + SHARE, :], g_p[:, :, lo : lo + SHARE].rearrange("p r i -> p i r"))

@@ -18,11 +18,7 @@ P = 128
 PACK = 4
 N = 512
 T = 2048
-CHUNK_COLS = ((0, 1024), (1024, 2048))
-QUANT_COLS = ((0, 512), (512, 1024), (1024, 1536), (1536, 1792), (1792, 2048))
-SCALAR_CHUNKS = (1,)
-LAST_ON_VECTOR = 960
-STORE_COLS = ((0, 512), (512, 1024), (1024, 1536), (1536, 1792), (1792, 2048))
+PAIR_COLS = ((0, 512), (512, 1280), (1280, 1536), (1536, 2048))
 
 FLOPS = 2 * 2 * 512 * 512 * 512
 
@@ -81,8 +77,6 @@ def tile_attend_gcentre_pl_kernel(tc, uT, vT, su, sv, y, offs, qoffs, out_0, out
 
         g_codes = tile([P, N], U32, "g_codes")
         g_scales = tile([P, N], U8, "g_scales")
-        nc.vector.memset(g_codes[:, N // 2 : N], 0)
-        nc.vector.memset(g_scales[:, N // 2 : N], 0)
 
         v_g = tile([P, PACK, N], BF16, "v_g")
         s_g = tile([P, N], F32, "s_g")
@@ -242,77 +236,114 @@ def tile_attend_gcentre_pl_kernel(tc, uT, vT, su, sv, y, offs, qoffs, out_0, out
                 )
         g_j = tile([P, N, PACK], BF16, "g_j", tag="v_d")
         out_rows = out_0.rearrange("(p t) c -> p t c", t=PACK)
-        last = PACK - 1
-        woven = [tile([P, hi - lo, PACK], BF16, "woven%d" % lo) for lo, hi in CHUNK_COLS]
-        du = [tile([P, N], F32, "du%d" % t, tag="y_sb%d" % t) for t in range(PACK)]
+        du_lo = [
+            [tile([P, H], F32, "du%d_%d" % (t, h), tag="v_d" if (t, h) == (1, 0) else None) for h in range(2)]
+            for t in range(2)
+        ]
+        du_banks = (("A0", "A1"), ("A2", "A3"))
 
-        def second_product(t, bank_tag, cols):
-            du_ps = bank("du_ps%d_%d" % (t, cols.start), bank_tag)
+        def second_product(t, cols, dst):
             rows = slice(t * P, (t + 1) * P)
             nc.tensor.matmul_mx(
-                du_ps[:], lhsT=vj_codes[:, rows].bitcast(E4M3), lhsT_scale=vj_scales[:, rows],
-                rhs=g_codes[:].bitcast(E5M2), rhs_scale=g_scales[:], start=True, stop=True,
+                dst, lhsT=vj_codes[:, rows].bitcast(E4M3), lhsT_scale=vj_scales[:, rows],
+                rhs=g_codes[:, cols].bitcast(E5M2), rhs_scale=g_scales[:, cols], start=True, stop=True,
             )
-            nc.scalar.copy(du[t][:, cols], du_ps[:, cols])
 
-        for h, SHARE in enumerate((144, 208)):
+        def places(t, h):
+            return out_win[t][:].indirect(item_list[:, h * H // 16 : (h + 1) * H // 16])
+
+        du_ps = []
+        for h, SHARE in enumerate((144, 256)):
             lo, hi = h * H, (h + 1) * H
             for r in range(PACK):
                 nc.vector.scalar_tensor_tensor(
                     g_p[:, r, lo:hi], c_half(h, r), col_mean[r][:], w[r][:, lo:hi], ALU.subtract, ALU.mult
                 )
-            nc.scalar.copy(g_j[:, lo + SHARE : hi, :], g_p[:, :, lo + SHARE : hi].rearrange("p r i -> p i r"))
+            if SHARE < H:
+                nc.scalar.copy(g_j[:, lo + SHARE : hi, :], g_p[:, :, lo + SHARE : hi].rearrange("p r i -> p i r"))
             nc.vector.tensor_copy(g_j[:, lo : lo + SHARE, :], g_p[:, :, lo : lo + SHARE].rearrange("p r i -> p i r"))
             nc.vector.quantize_mx(
                 out=g_codes[:, lo:hi].bitcast(E5M2), scales=g_scales[:, lo:hi],
                 in_=g_j[:, lo:hi, :].rearrange("p i r -> p (i r)"),
             )
-            second_product(0, "A%d" % h, slice(lo, hi))
-        for t in range(1, PACK):
-            second_product(t, "A%d" % ((t + 1) % PACK), slice(0, N))
-        for t in range(PACK):
-            if t == 0:
-                for h in range(2):
-                    nc.vector.tensor_copy(
-                        out_win[t][:].indirect(item_list[:, h * H // 16 : (h + 1) * H // 16]), du[t][:, h * H : (h + 1) * H]
-                    )
+            banks = [bank("du_ps%d_%d" % (h, k), du_banks[h][k]) for k in range(2)]
+            du_ps.append(banks)
+            second_product(0, slice(lo, hi), banks[0][:, 0:H])
+            second_product(1, slice(lo, hi), banks[1][:, 0:H])
+            nc.scalar.copy(du_lo[0][h][:], banks[0][:, 0:H])
+            nc.scalar.activation(places(0, h), du_lo[0][h][:], ACT.Copy)
+        hi_ps = [bank("hi_ps%d" % k, "C%d" % k) for k in range(2)]
+        for k in range(2):
+            second_product(2 + k, slice(0, N), hi_ps[k][:])
+        nc.sync.dma_start(out_rows[:, 0, :], out_win[0][:])
+        du_hi = [tile([P, N], F32, "du_hi%d" % k, tag=("du0_1", "du_last")[k]) for k in range(2)]
+        nc.vector.tensor_copy(du_lo[1][0][:], du_ps[0][1][:, 0:H])
+        nc.vector.tensor_copy(places(1, 0), du_lo[1][0][:])
+        nc.vector.tensor_copy(du_lo[1][1][:], du_ps[1][1][:, 0:H])
+        nc.vector.tensor_copy(du_hi[1][:], hi_ps[1][:])
+        nc.vector.tensor_copy(places(1, 1), du_lo[1][1][:])
+        nc.sync.dma_start(out_rows[:, 1, :], out_win[1][:])
+        nc.scalar.copy(du_hi[0][:], hi_ps[0][:])
+        for h in range(2):
+            nc.scalar.activation(places(2, h), du_hi[0][:, h * H : (h + 1) * H], ACT.Copy)
+        nc.sync.dma_start(out_rows[:, 2, :], out_win[2][:])
+        nc.vector.tensor_copy(out_win[3][:].indirect(item_list[:]), du_hi[1][:])
+        nc.scalar.dma_start(out_rows[:, 3, :], out_win[3][:])
+
+        pairs = [
+            tile([P, 2, hi - lo, 2], BF16, "pairs%d" % lo)
+            for c, (lo, hi) in enumerate(PAIR_COLS)
+        ]
+
+        def round_plane(eng, c, t, lo, hi):
+            base = PAIR_COLS[c][0]
+            dst, src = pairs[c][:, t // 2, lo - base : hi - base, t % 2], out_win[t][:, lo:hi]
+            if eng == "gpsimd":
+                nc.gpsimd.tensor_scalar(dst, src, 1.0, 0.0, ALU.mult, ALU.add)
+            elif eng == "scalar":
+                nc.scalar.copy(dst, src)
             else:
-                nc.vector.tensor_copy(out_win[t][:].indirect(item_list[:]), du[t][:])
-            (nc.sync if t < last else nc.scalar).dma_start(out_rows[:, t, :], out_win[t][:])
-            for c, (lo, hi) in enumerate(CHUNK_COLS):
-                src = out_win[t][:, lo:hi]
-                if c in SCALAR_CHUNKS and t < last:
-                    nc.scalar.copy(woven[c][:, :, t], src)
-                elif c in SCALAR_CHUNKS:
-                    for first, end in QUANT_COLS[2:]:
-                        nc.scalar.copy(woven[c][:, first - lo : end - lo, t], src[:, first - lo : end - lo])
-                elif t < last - 1:
-                    nc.gpsimd.tensor_scalar(woven[c][:, :, t], src, 1.0, 0.0, ALU.mult, ALU.add)
-                elif t < last:
-                    nc.gpsimd.tensor_scalar(
-                        woven[c][:, :, t : t + 2], src.unsqueeze(2).to_broadcast([P, hi - lo, 2]), 1.0, 0.0, ALU.mult, ALU.add
-                    )
-                else:
-                    cut = LAST_ON_VECTOR
-                    nc.vector.tensor_copy(woven[c][:, 0:N, t], src[:, 0:N])
-                    nc.vector.tensor_copy(woven[c][:, N:cut, t], src[:, N:cut])
-                    nc.scalar.copy(woven[c][:, cut:, t], src[:, cut:])
+                nc.vector.tensor_copy(dst, src)
+
+        def weave(c, lo, hi, tag):
+            base = PAIR_COLS[c][0]
+            words_in = pairs[c][:].rearrange("p u c e -> p u (c e)").bitcast(F32)[:, :, lo - base : hi - base]
+            woven = tile([P, hi - lo, 2], F32, "woven%d" % lo, tag=tag)
+            nc.vector.tensor_copy(woven[:], words_in.rearrange("p u c -> p c u"))
+            return woven, lo, hi
 
         out_codes = tile([P, T], U32, "out_codes")
         out_scales = tile([P, T // 2], U8, "out_scales")
         words = out_1[0].rearrange("p c l -> p (c l)").bitcast(I32)
-        for lo, hi in QUANT_COLS:
-            c = [k for k, (first, end) in enumerate(CHUNK_COLS) if first <= lo < end][0]
-            base = CHUNK_COLS[c][0]
-            cols = slice(lo, hi)
+
+        def quantize_out(woven, lo, hi):
             nc.vector.quantize_mx(
-                out=out_codes[:, cols].bitcast(E4M3), scales=out_scales[PACK * (lo // (T // 2)) : P, lo % (T // 2) : lo % (T // 2) + hi - lo],
-                in_=woven[c][:, lo - base : hi - base, :].rearrange("p c t -> p (c t)"),
+                out=out_codes[:, lo:hi].bitcast(E4M3),
+                scales=out_scales[PACK * (lo // (T // 2)) : P, lo % (T // 2) : lo % (T // 2) + hi - lo],
+                in_=woven[:].rearrange("p c u -> p (c u)").bitcast(BF16),
             )
-            for first, end in STORE_COLS:
-                if end == hi:
-                    nc.sync.dma_start(words[:, first:end], out_codes[:, first:end].bitcast(I32))
+            nc.sync.dma_start(words[:, lo:hi], out_codes[:, lo:hi].bitcast(I32))
+
+        for t in range(2):
+            for c in range(2):
+                round_plane("gpsimd", c, t, *PAIR_COLS[c])
+        for t in (3, 2, 0, 1):
+            round_plane("vector", 3, t, *PAIR_COLS[3])
+        for c in range(2):
+            for t in (2, 3):
+                round_plane("scalar", c, t, *PAIR_COLS[c])
+        for t in (3, 2, 0, 1):
+            round_plane("scalar", 2, t, *PAIR_COLS[2])
+        w_own = weave(3, 1536, 2048, "woven_a")
+        w0 = weave(0, 0, 512, "woven_b")
+        quantize_out(*w_own)
+        quantize_out(*w0)
+        w1 = weave(1, 512, 1024, "woven_b")
+        w2 = weave(1, 1024, 1280, "woven_a")
+        quantize_out(*w1)
+        w3 = weave(2, 1280, 1536, "woven_b")
+        quantize_out(*w2)
+        quantize_out(*w3)
         scale_rows = out_2[0].bitcast(I32).rearrange("(q r) (a c) -> q a r c", r=PACK, a=2)
         for Q in range(PACK):
-            eng = nc.sync if Q % 2 == 0 else nc.scalar
-            eng.dma_start(scale_rows[Q], out_scales[32 * Q : 32 * Q + 2 * PACK, :].bitcast(I32))
+            (nc.sync if Q % 2 == 0 else nc.scalar).dma_start(scale_rows[Q], out_scales[32 * Q : 32 * Q + 2 * PACK, :].bitcast(I32))

@@ -18,7 +18,6 @@ P = 128
 PACK = 4
 N = 512
 T = 2048
-PAIR_COLS = ((0, 512), (512, 1280), (1280, 1536), (1536, 2048))
 
 FLOPS = 2 * 2 * 512 * 512 * 512
 
@@ -276,7 +275,7 @@ def tile_attend_gcentre_pl_kernel(tc, uT, vT, su, sv, y, offs, qoffs, out_0, out
         for k in range(2):
             second_product(2 + k, slice(0, N), hi_ps[k][:])
         nc.sync.dma_start(out_rows[:, 0, :], out_win[0][:])
-        du_hi = [tile([P, N], F32, "du_hi%d" % k, tag=("du0_1", "du_last")[k]) for k in range(2)]
+        du_hi = [tile([P, N], F32, "du_hi%d" % k, tag=("du_third", "du_last")[k]) for k in range(2)]
         nc.vector.tensor_copy(du_lo[1][0][:], du_ps[0][1][:, 0:H])
         nc.vector.tensor_copy(places(1, 0), du_lo[1][0][:])
         nc.vector.tensor_copy(du_lo[1][1][:], du_ps[1][1][:, 0:H])
@@ -286,18 +285,15 @@ def tile_attend_gcentre_pl_kernel(tc, uT, vT, su, sv, y, offs, qoffs, out_0, out
         nc.scalar.copy(du_hi[0][:], hi_ps[0][:])
         for h in range(2):
             nc.scalar.activation(places(2, h), du_hi[0][:, h * H : (h + 1) * H], ACT.Copy)
-        nc.sync.dma_start(out_rows[:, 2, :], out_win[2][:])
+        nc.scalar.dma_start(out_rows[:, 2, :], out_win[2][:])
         nc.vector.tensor_copy(out_win[3][:].indirect(item_list[:]), du_hi[1][:])
-        nc.scalar.dma_start(out_rows[:, 3, :], out_win[3][:])
+        nc.sync.dma_start(out_rows[:, 3, :], out_win[3][:])
 
-        pairs = [
-            tile([P, 2, hi - lo, 2], BF16, "pairs%d" % lo)
-            for c, (lo, hi) in enumerate(PAIR_COLS)
-        ]
+        rounded = tile([P, PACK, T], BF16, "rounded")
+        woven = tile([P, T, PACK], BF16, "woven")
 
-        def round_plane(eng, c, t, lo, hi):
-            base = PAIR_COLS[c][0]
-            dst, src = pairs[c][:, t // 2, lo - base : hi - base, t % 2], out_win[t][:, lo:hi]
+        def round_plane(eng, t, lo, hi):
+            dst, src = rounded[:, t, lo:hi], out_win[t][:, lo:hi]
             if eng == "gpsimd":
                 nc.gpsimd.tensor_scalar(dst, src, 1.0, 0.0, ALU.mult, ALU.add)
             elif eng == "scalar":
@@ -305,45 +301,38 @@ def tile_attend_gcentre_pl_kernel(tc, uT, vT, su, sv, y, offs, qoffs, out_0, out
             else:
                 nc.vector.tensor_copy(dst, src)
 
-        def weave(c, lo, hi, tag):
-            base = PAIR_COLS[c][0]
-            words_in = pairs[c][:].rearrange("p u c e -> p u (c e)").bitcast(F32)[:, :, lo - base : hi - base]
-            woven = tile([P, hi - lo, 2], F32, "woven%d" % lo, tag=tag)
-            nc.vector.tensor_copy(woven[:], words_in.rearrange("p u c -> p c u"))
-            return woven, lo, hi
+        def weave(eng, lo, hi):
+            dst = woven[:, lo:hi, :]
+            src = rounded[:, :, lo:hi].rearrange("p t c -> p c t")
+            if eng == "scalar":
+                nc.scalar.copy(dst, src)
+            else:
+                nc.vector.tensor_copy(dst, src)
 
         out_codes = tile([P, T], U32, "out_codes")
         out_scales = tile([P, T // 2], U8, "out_scales")
         words = out_1[0].rearrange("p c l -> p (c l)").bitcast(I32)
 
-        def quantize_out(woven, lo, hi):
+        def quantize_out(lo, hi):
             nc.vector.quantize_mx(
                 out=out_codes[:, lo:hi].bitcast(E4M3),
                 scales=out_scales[PACK * (lo // (T // 2)) : P, lo % (T // 2) : lo % (T // 2) + hi - lo],
-                in_=woven[:].rearrange("p c u -> p (c u)").bitcast(BF16),
+                in_=woven[:, lo:hi, :].rearrange("p c t -> p (c t)"),
             )
             nc.sync.dma_start(words[:, lo:hi], out_codes[:, lo:hi].bitcast(I32))
 
-        for t in range(2):
-            for c in range(2):
-                round_plane("gpsimd", c, t, *PAIR_COLS[c])
-        for t in (3, 2, 0, 1):
-            round_plane("vector", 3, t, *PAIR_COLS[3])
-        for c in range(2):
-            for t in (2, 3):
-                round_plane("scalar", c, t, *PAIR_COLS[c])
-        for t in (3, 2, 0, 1):
-            round_plane("scalar", 2, t, *PAIR_COLS[2])
-        w_own = weave(3, 1536, 2048, "woven_a")
-        w0 = weave(0, 0, 512, "woven_b")
-        quantize_out(*w_own)
-        quantize_out(*w0)
-        w1 = weave(1, 512, 1024, "woven_b")
-        w2 = weave(1, 1024, 1280, "woven_a")
-        quantize_out(*w1)
-        w3 = weave(2, 1280, 1536, "woven_b")
-        quantize_out(*w2)
-        quantize_out(*w3)
+        round_plane("gpsimd", 0, 0, 2048)
+        round_plane("gpsimd", 1, 0, 2048)
+        round_plane("vector", 3, 0, 2048)
+        round_plane("scalar", 2, 0, 640)
+        round_plane("scalar", 2, 640, 2048)
+        weave("scalar", 1216, 1536)
+        weave("scalar", 1536, 1792)
+        weave("scalar", 1792, 2048)
+        weave("vector", 0, 640)
+        weave("vector", 640, 1216)
+        for lo, hi in ((0, 512), (512, 1024), (1024, 1536), (1536, 1792), (1792, 2048)):
+            quantize_out(lo, hi)
         scale_rows = out_2[0].bitcast(I32).rearrange("(q r) (a c) -> q a r c", r=PACK, a=2)
         for Q in range(PACK):
             (nc.sync if Q % 2 == 0 else nc.scalar).dma_start(scale_rows[Q], out_scales[32 * Q : 32 * Q + 2 * PACK, :].bitcast(I32))

@@ -19,6 +19,8 @@ PACK = 4
 N = 512
 T = 2048
 
+OUT_COLS = ((0, 512), (512, 1024), (1024, 1536), (1536, 1792), (1792, 2048))
+ROUND_COLS = ((0, 512), (512, 1536), (1536, 2048))
 FLOPS = 2 * 2 * 512 * 512 * 512
 
 
@@ -289,11 +291,16 @@ def tile_attend_gcentre_pl_kernel(tc, uT, vT, su, sv, y, offs, qoffs, out_0, out
         nc.vector.tensor_copy(out_win[3][:].indirect(item_list[:]), du_hi[1][:])
         nc.sync.dma_start(out_rows[:, 3, :], out_win[3][:])
 
-        rounded = tile([P, PACK, T], BF16, "rounded")
-        woven = tile([P, T, PACK], BF16, "woven")
+        rounded = [tile([P, PACK, hi - lo], BF16, "rounded%d" % lo) for lo, hi in ROUND_COLS]
+
+        def rounded_cols(lo, hi):
+            c = [k for k, (first, end) in enumerate(ROUND_COLS) if first <= lo < end][0]
+            return rounded[c][:, :, lo - ROUND_COLS[c][0] : hi - ROUND_COLS[c][0]]
+
+        woven = {lo: tile([P, hi - lo, PACK], BF16, "woven%d" % lo) for lo, hi in OUT_COLS}
 
         def round_plane(eng, t, lo, hi):
-            dst, src = rounded[:, t, lo:hi], out_win[t][:, lo:hi]
+            dst, src = rounded_cols(lo, hi)[:, t, :], out_win[t][:, lo:hi]
             if eng == "gpsimd":
                 nc.gpsimd.tensor_scalar(dst, src, 1.0, 0.0, ALU.mult, ALU.add)
             elif eng == "scalar":
@@ -302,8 +309,8 @@ def tile_attend_gcentre_pl_kernel(tc, uT, vT, su, sv, y, offs, qoffs, out_0, out
                 nc.vector.tensor_copy(dst, src)
 
         def weave(eng, lo, hi):
-            dst = woven[:, lo:hi, :]
-            src = rounded[:, :, lo:hi].rearrange("p t c -> p c t")
+            dst = woven[lo][:].rearrange("p (c i) t -> p c t i", i=PACK)
+            src = rounded_cols(lo, hi).rearrange("p t (c i) -> p c t i", i=PACK)
             if eng == "scalar":
                 nc.scalar.copy(dst, src)
             else:
@@ -317,21 +324,24 @@ def tile_attend_gcentre_pl_kernel(tc, uT, vT, su, sv, y, offs, qoffs, out_0, out
             nc.vector.quantize_mx(
                 out=out_codes[:, lo:hi].bitcast(E4M3),
                 scales=out_scales[PACK * (lo // (T // 2)) : P, lo % (T // 2) : lo % (T // 2) + hi - lo],
-                in_=woven[:, lo:hi, :].rearrange("p c t -> p (c t)"),
+                in_=woven[lo][:].rearrange("p c t -> p (c t)"),
             )
             nc.sync.dma_start(words[:, lo:hi], out_codes[:, lo:hi].bitcast(I32))
 
-        round_plane("gpsimd", 0, 0, 2048)
-        round_plane("gpsimd", 1, 0, 2048)
-        round_plane("vector", 3, 0, 2048)
-        round_plane("scalar", 2, 0, 640)
-        round_plane("scalar", 2, 640, 2048)
-        weave("scalar", 1216, 1536)
-        weave("scalar", 1536, 1792)
-        weave("scalar", 1792, 2048)
-        weave("vector", 0, 640)
-        weave("vector", 640, 1216)
-        for lo, hi in ((0, 512), (512, 1024), (1024, 1536), (1536, 1792), (1792, 2048)):
+        round_plane("gpsimd", 0, 0, 512)
+        round_plane("gpsimd", 0, 512, 896)
+        for lo, hi in ROUND_COLS:
+            round_plane("gpsimd", 1, lo, hi)
+        round_plane("vector", 3, 0, 512)
+        round_plane("vector", 3, 512, 1536)
+        round_plane("scalar", 2, 0, 512)
+        round_plane("scalar", 0, 896, 1536)
+        round_plane("scalar", 2, 512, 1536)
+        for t in (0, 2, 3):
+            round_plane("scalar", t, 1536, 2048)
+        for lo, hi in OUT_COLS:
+            weave("vector" if hi <= 1536 else "scalar", lo, hi)
+        for lo, hi in OUT_COLS:
             quantize_out(lo, hi)
         scale_rows = out_2[0].bitcast(I32).rearrange("(q r) (a c) -> q a r c", r=PACK, a=2)
         for Q in range(PACK):

@@ -169,7 +169,6 @@ def tile_attend_gcentre_pl_kernel(tc, uT, vT, su, sv, y, offs, qoffs, out_0, out
         def c_block(q, r):
             return c_half(q // 2, r)[:, (q % 2) * P : (q % 2 + 1) * P]
 
-        EARLY = 3
         neg_y, neg_sum = [], []
         for q in range(PACK):
             ny = tile([P, PACK, P], F32, "neg_y%d" % q)
@@ -179,12 +178,11 @@ def tile_attend_gcentre_pl_kernel(tc, uT, vT, su, sv, y, offs, qoffs, out_0, out
             )
             neg_y.append(ny)
             neg_sum.append(ns)
-            if q < EARLY:
-                for r in range(PACK):
-                    nc.tensor.matmul(
-                        c_block(q, r), lhsT=y_sb[q][:, r:N:PACK] if q == 0 else ny[:, r, :], rhs=ident[:],
-                        start=(q % 2 == 0 and r % 2 == 0), stop=False, is_transpose=True,
-                    )
+            for r in range(PACK):
+                nc.tensor.matmul(
+                    c_block(q, r), lhsT=ny[:, r, :], rhs=ident[:],
+                    start=(q % 2 == 0 and r % 2 == 0), stop=False, is_transpose=True,
+                )
 
         b = [tile([P, N], F32, "b%d" % q) for q in range(PACK)]
         row_sum = [tile([P, 1], F32, "row_sum%d" % q) for q in range(PACK)]
@@ -200,24 +198,18 @@ def tile_attend_gcentre_pl_kernel(tc, uT, vT, su, sv, y, offs, qoffs, out_0, out
             if q > 0:
                 row_shift(q - 1)
         row_shift(PACK - 1)
+        def add_turned(q, r, src, stop):
+            nc.tensor.matmul(c_block(q, r), lhsT=src, rhs=ident[:], start=False, stop=stop, is_transpose=True)
+
         for q in range(PACK):
-            if q < EARLY:
+            if q < 2:
                 nc.scalar.activation(b[q][:], b[q][:], ACT.Identity, scale=1.0, bias=shift[q][:])
             else:
-                for h in range(2):
-                    half = slice(h * H, (h + 1) * H)
-                    nc.vector.scalar_tensor_tensor(
-                        b[q][:, half], b[q][:, half], shift[q][:],
-                        neg_y[q][:].rearrange("p r s -> p (r s)")[:, half], ALU.add, ALU.add,
-                    )
-        turns = [(q, r) for q in range(PACK) for r in range(PACK)]
-        for q, r in turns:
-            nc.tensor.matmul(
-                c_block(q, r), lhsT=b[q][:, r * P : (r + 1) * P], rhs=ident[:],
-                start=False, stop=(q % 2 == 1 and r % 2 == 1), is_transpose=True,
-            )
+                nc.vector.tensor_scalar_add(b[q][:], b[q][:], shift[q][:])
+            for r in range(PACK):
+                add_turned(q, r, b[q][:, r * P : (r + 1) * P], q % 2 == 1 and r % 2 == 1)
 
-        vj_codes, vj_scales = quantize(v_j[:].rearrange("p t d r -> p (t d r)"), "vj", E4M3, tag="neg_y3")
+        vj_codes, vj_scales = quantize(v_j[:].rearrange("p t d r -> p (t d r)"), "vj", E4M3, tag="shift3")
         g_p = tile([P, PACK, N], BF16, "g_p", tag="v_g")
         col_mean = [tile([P, 1], F32, "col_mean%d" % r) for r in range(PACK)]
         part = [tile([P, 1], F32, "part%d" % r) for r in range(PACK)]

@@ -230,7 +230,7 @@ def tile_attend_gcentre_pl_kernel(tc, uT, vT, su, sv, y, offs, qoffs, out_0, out
         g_j = tile([P, N, PACK], BF16, "g_j", tag="v_d")
         out_rows = out_0.rearrange("(p t) c -> p t c", t=PACK)
         du_lo = [
-            [tile([P, H], F32, "du%d_%d" % (t, h), tag="v_d" if (t, h) == (1, 0) else None) for h in range(2)]
+            [tile([P, H], F32, "du%d_%d" % (t, h), tag=None) for h in range(2)]
             for t in range(2)
         ]
         du_banks = (("A0", "A1"), ("A2", "A3"))
@@ -264,13 +264,14 @@ def tile_attend_gcentre_pl_kernel(tc, uT, vT, su, sv, y, offs, qoffs, out_0, out
             second_product(0, slice(lo, hi), banks[0][:, 0:H])
             second_product(1, slice(lo, hi), banks[1][:, 0:H])
             nc.scalar.copy(du_lo[0][h][:], banks[0][:, 0:H])
+            if h == 0:
+                nc.scalar.copy(du_lo[1][h][:], banks[1][:, 0:H])
             nc.scalar.activation(places(0, h), du_lo[0][h][:], ACT.Copy)
         hi_ps = [bank("hi_ps%d" % k, "C%d" % k) for k in range(2)]
         for k in range(2):
             second_product(2 + k, slice(0, N), hi_ps[k][:])
         nc.sync.dma_start(out_rows[:, 0, :], out_win[0][:])
         du_hi = [tile([P, N], F32, "du_hi%d" % k, tag=("du_third", "du_last")[k]) for k in range(2)]
-        nc.vector.tensor_copy(du_lo[1][0][:], du_ps[0][1][:, 0:H])
         nc.vector.tensor_copy(places(1, 0), du_lo[1][0][:])
         nc.vector.tensor_copy(du_lo[1][1][:], du_ps[1][1][:, 0:H])
         nc.vector.tensor_copy(du_hi[1][:], hi_ps[1][:])
@@ -283,7 +284,9 @@ def tile_attend_gcentre_pl_kernel(tc, uT, vT, su, sv, y, offs, qoffs, out_0, out
         nc.vector.tensor_copy(out_win[3][:].indirect(item_list[:]), du_hi[1][:])
         nc.sync.dma_start(out_rows[:, 3, :], out_win[3][:])
 
-        rounded = [tile([P, PACK, hi - lo], BF16, "rounded%d" % lo) for lo, hi in ROUND_COLS]
+        rounded = [
+            tile([P, PACK, hi - lo], BF16, "rounded%d" % lo, tag="du_third" if hi == T else None) for lo, hi in ROUND_COLS
+        ]
 
         def rounded_cols(lo, hi):
             c = [k for k, (first, end) in enumerate(ROUND_COLS) if first <= lo < end][0]
@@ -304,7 +307,7 @@ def tile_attend_gcentre_pl_kernel(tc, uT, vT, su, sv, y, offs, qoffs, out_0, out
             dst = woven[lo][:].rearrange("p (c i) t -> p c t i", i=PACK)
             src = rounded_cols(lo, hi).rearrange("p t (c i) -> p c t i", i=PACK)
             if eng == "scalar":
-                nc.scalar.copy(dst, src)
+                nc.scalar.copy(woven[lo][:], rounded_cols(lo, hi).rearrange("p t c -> p c t"))
             else:
                 nc.vector.tensor_copy(dst, src)
 
@@ -321,16 +324,16 @@ def tile_attend_gcentre_pl_kernel(tc, uT, vT, su, sv, y, offs, qoffs, out_0, out
             nc.sync.dma_start(words[:, lo:hi], out_codes[:, lo:hi].bitcast(I32))
 
         round_plane("gpsimd", 0, 0, 512)
-        round_plane("gpsimd", 0, 512, 896)
-        for lo, hi in ROUND_COLS:
+        round_plane("gpsimd", 0, 512, 1152)
+        for lo, hi in ROUND_COLS[:2]:
             round_plane("gpsimd", 1, lo, hi)
-        round_plane("vector", 3, 0, 512)
-        round_plane("vector", 3, 512, 1536)
+        for lo, hi in ROUND_COLS[:2]:
+            round_plane("vector", 3, lo, hi)
         round_plane("scalar", 2, 0, 512)
-        round_plane("scalar", 0, 896, 1536)
+        round_plane("scalar", 0, 1152, 1536)
         round_plane("scalar", 2, 512, 1536)
-        for t in (0, 2, 3):
-            round_plane("scalar", t, 1536, 2048)
+        for t in range(PACK):
+            round_plane("scalar", t, *ROUND_COLS[2])
         for lo, hi in OUT_COLS:
             weave("vector" if hi <= 1536 else "scalar", lo, hi)
         for lo, hi in OUT_COLS:

from contextlib import ExitStack

import concourse.mybir as mybir
from concourse.masks import make_identity

F32 = mybir.dt.float32
BF16 = mybir.dt.bfloat16
U32 = mybir.dt.uint32
I32 = mybir.dt.int32
U16 = mybir.dt.uint16
U8 = mybir.dt.uint8
E4M3 = mybir.dt.float8_e4m3fn_x4
E5M2 = mybir.dt.float8_e5m2_x4
ACT = mybir.ActivationFunctionType
ALU = mybir.AluOpType

P = 128
PACK = 4
N = 512
T = 2048

OUT_COLS = ((0, 512), (512, 1024), (1024, 1536), (1536, 1792), (1792, 2048))
ROUND_COLS = ((0, 512), (512, 1536), (1536, 2048))
FLOPS = 2 * 2 * 512 * 512 * 512


def tile_attend_gcentre_pl_kernel(tc, uT, vT, su, sv, y, offs, qoffs, out_0, out_1, out_2):
    nc = tc.nc
    with ExitStack() as ctx:
        held = ctx.enter_context(tc.tile_pool(name="held", bufs=1))
        sb = ctx.enter_context(tc.tile_pool(name="sb", bufs=1))
        psum = ctx.enter_context(tc.psum_pool(name="psum", bufs=1))

        def tile(shape, dtype, name, tag=None):
            return sb.tile(shape, dtype, name=name, tag=tag or name, align_bytes=64)

        def bank(name, tag):
            return psum.tile([P, N], F32, name=name, tag=tag)

        item_list = held.tile([P, N // 16], U16, name="item_list")
        partner_list = held.tile([P, N // 16], U16, name="partner_list")

        u_rows = uT.rearrange("(p t) c -> p t c", t=PACK)
        v_rows = vT.rearrange("(p t) c -> p t c", t=PACK)
        v_win = [tile([P, T], F32, "v_win%d" % t) for t in range(PACK)]
        u_win = [tile([P, T], F32, "u_win%d" % t) for t in range(PACK)]
        y_sb = [tile([P, N], F32, "y_sb%d" % q) for q in range(PACK)]
        su_win = tile([P, T], F32, "su_win")
        sv_win = tile([P, T], F32, "sv_win")
        RUN = T // P
        sv_run = tile([P, RUN], F32, "sv_run")
        su_run = tile([P, RUN], F32, "su_run")
        nc.sync.dma_start(sv_run[:], sv[0].rearrange("(p k) -> p k", k=RUN))
        nc.sync.dma_start(su_run[:], su[0].rearrange("(p k) -> p k", k=RUN))
        nc.sync.dma_start(partner_list[:], qoffs)
        nc.sync.dma_start(v_win[0][:], v_rows[:, 0, :])
        nc.sync.dma_start(item_list[:], offs)
        for t in range(1, PACK):
            nc.sync.dma_start(v_win[t][:], v_rows[:, t, :])
        for t in range(PACK):
            nc.sync.dma_start(u_win[t][:], u_rows[:, t, :])
        for q in range(PACK):
            nc.sync.dma_start(y_sb[q][:], y[q * P : (q + 1) * P, :])

        ident = tile([P, P], F32, "ident")
        make_identity(nc, ident[:])

        for run, win, tagc in ((sv_run, sv_win, "A"), (su_run, su_win, "C")):
            for bk in range(PACK):
                sp = bank("spread%s%d" % (tagc, bk), "%s%d" % (tagc, bk))
                for k in range(PACK):
                    col = PACK * bk + k
                    nc.tensor.transpose(sp[:, k * P : (k + 1) * P], run[:, col : col + 1].to_broadcast([P, P]), ident[:])
                nc.scalar.copy(
                    win[:].rearrange("m (p k) -> m p k", k=RUN)[:, :, PACK * bk : PACK * (bk + 1)],
                    sp[:].rearrange("m (k p) -> m p k", k=PACK),
                )

        g_codes = tile([P, N], U32, "g_codes")
        g_scales = tile([P, N], U8, "g_scales")

        v_g = tile([P, PACK, N], BF16, "v_g")
        s_g = tile([P, N], F32, "s_g")
        t_g = tile([P, N], F32, "t_g")
        for t in range(PACK):
            nc.vector.tensor_copy(v_g[:, t, :], v_win[t][:].indirect(partner_list[:]))
            if t == 1:
                nc.vector.tensor_copy(t_g[:], sv_win[:].indirect(partner_list[:]))
            if t == 2:
                nc.vector.tensor_copy(s_g[:], su_win[:].indirect(item_list[:]))

        out_win = [tile([P, T], F32, "out_win%d" % t, tag="v_win%d" % t) for t in range(PACK)]
        for t in range(PACK):
            nc.gpsimd.memset(out_win[t][:], 0.0)

        t_row = tile([P, N], F32, "t_row")
        nc.scalar.copy(t_row[:].rearrange("p (r s) -> p s r", r=PACK), t_g[:].rearrange("p (s r) -> p s r", r=PACK))
        t_ps = bank("t_ps", "A2")
        s_ps = bank("s_ps", "A3")
        for r in range(PACK):
            nc.tensor.transpose(t_ps[:, r * P : (r + 1) * P], t_row[:, r * P : (r + 1) * P], ident[:])
        for q in range(PACK):
            nc.tensor.transpose(s_ps[:, q * P : (q + 1) * P], s_g[:, q * P : (q + 1) * P], ident[:])
        t_col = tile([P, PACK], F32, "t_col")
        s_col = tile([P, PACK], F32, "s_col")
        nc.scalar.activation(t_col[:], t_ps[:, 0:N:P], ACT.Copy, scale=-1.0)
        nc.scalar.activation(s_col[:], s_ps[:, 0:N:P], ACT.Copy, scale=-1.0)

        v_d = tile([P, N, PACK], BF16, "v_d")
        nc.scalar.copy(
            v_d[:].rearrange("p (r s) t -> p s r t", r=PACK),
            v_g[:].rearrange("p t (s r) -> p s r t", r=PACK),
        )
        v_words = v_d[:].rearrange("p j t -> p (j t)").bitcast(F32)
        v_j = tile([P, PACK, P, PACK], BF16, "v_j")
        for h in range(2):
            vt_ps = bank("vt_ps%d" % h, "A%d" % h)
            for r in range(PACK):
                nc.tensor.transpose(
                    vt_ps[:, r * P : (r + 1) * P], v_words[:, 2 * r * P + h : 2 * (r + 1) * P : 2], ident[:]
                )
            nc.scalar.copy(
                v_j[:, 2 * h : 2 * h + 2, :, :],
                vt_ps[:].bitcast(BF16).rearrange("p (r d e) -> p e d r", r=PACK, e=2),
            )


        def quantize(src, name, fmt, tag=None):
            codes = tile([P, N], U32, name + "_codes", tag=tag)
            scales = tile([P, N], U8, name + "_scales")
            nc.vector.quantize_mx(out=codes[:].bitcast(fmt), scales=scales[:], in_=src)
            return codes, scales

        u_d = tile([P, N, PACK], BF16, "u_d")
        nc.vector.tensor_copy(u_d[:, :, 0], u_win[0][:].indirect(item_list[:]))
        vd_codes, vd_scales = quantize(v_d[:].rearrange("p j t -> p (j t)"), "vd", E4M3)
        nc.vector.tensor_copy(u_d[:, :, 1], u_win[1][:].indirect(item_list[:]))
        nc.vector.tensor_copy(u_d[:, :, 2], u_win[2][:].indirect(item_list[:]))
        H = N // 2
        ud_codes = [tile([P, H], U32, "ud_codes%d" % h) for h in range(2)]
        ud_scales = [tile([P, H], U8, "ud_scales%d" % h) for h in range(2)]
        for h in range(2):
            nc.vector.tensor_copy(
                u_d[:, h * H : (h + 1) * H, 3], u_win[3][:].indirect(item_list[:, h * H // 16 : (h + 1) * H // 16])
            )
            nc.vector.quantize_mx(
                out=ud_codes[h][:].bitcast(E4M3), scales=ud_scales[h][:],
                in_=u_d[:, h * H : (h + 1) * H, :].rearrange("p i t -> p (i t)"),
            )

        w_all = tile([P, PACK, N], F32, "w_all", tag="u_d")
        w = [w_all[:, r, :] for r in range(PACK)]
        for r in range(PACK):
            nc.gpsimd.tensor_scalar(w[r], s_g[:], t_col[:, r : r + 1], 0.0, ALU.mult, ALU.add)

        a_ps = [bank("a_ps%d" % q, "A%d" % q) for q in range(PACK)]
        for q in range(PACK):
            cols = slice((q % 2) * P, (q % 2 + 1) * P)
            nc.tensor.matmul_mx(
                a_ps[q][:], lhsT=ud_codes[q // 2][:, cols].bitcast(E4M3), lhsT_scale=ud_scales[q // 2][:, cols],
                rhs=vd_codes[:].bitcast(E4M3), rhs_scale=vd_scales[:], start=True, stop=True,
            )

        c_ps = [[bank("c_ps%d%d" % (h, k), "C%d" % (2 * h + k)) for k in range(2)] for h in range(2)]

        def c_half(h, r):
            return c_ps[h][r // 2][:, (r % 2) * H : (r % 2 + 1) * H]

        def c_block(q, r):
            return c_half(q // 2, r)[:, (q % 2) * P : (q % 2 + 1) * P]

        neg_y, neg_sum = [], []
        for q in range(PACK):
            ny = tile([P, PACK, P], F32, "neg_y%d" % q)
            ns = tile([P, 1], F32, "neg_sum%d" % q)
            nc.scalar.activation(
                ny[:].rearrange("p r s -> p s r"), y_sb[q][:].rearrange("p (s r) -> p s r", r=PACK), ACT.Copy, accum_out=ns[:]
            )
            neg_y.append(ny)
            neg_sum.append(ns)
            for r in range(PACK):
                nc.tensor.matmul(
                    c_block(q, r), lhsT=ny[:, r, :], rhs=ident[:],
                    start=(q % 2 == 0 and r % 2 == 0), stop=False, is_transpose=True,
                )

        b = [tile([P, N], F32, "b%d" % q) for q in range(PACK)]
        row_sum = [tile([P, 1], F32, "row_sum%d" % q) for q in range(PACK)]
        shift = [tile([P, 1], F32, "shift%d" % q) for q in range(PACK)]

        def row_shift(q):
            nc.vector.tensor_scalar(shift[q][:], row_sum[q][:], neg_sum[q][:], -1.0 / N, ALU.add, ALU.mult)

        for q in range(PACK):
            nc.vector.scalar_tensor_tensor(
                b[q][:], a_ps[q][:], s_col[:, q : q + 1], t_row[:], ALU.mult, ALU.mult, accum_out=row_sum[q][:]
            )
            if q > 0:
                row_shift(q - 1)
        row_shift(PACK - 1)
        def add_turned(q, r, src, stop):
            nc.tensor.matmul(c_block(q, r), lhsT=src, rhs=ident[:], start=False, stop=stop, is_transpose=True)

        for q in range(PACK):
            if q < 2:
                nc.scalar.activation(b[q][:], b[q][:], ACT.Identity, scale=1.0, bias=shift[q][:])
            else:
                nc.vector.tensor_scalar_add(b[q][:], b[q][:], shift[q][:])
            for r in range(PACK):
                add_turned(q, r, b[q][:, r * P : (r + 1) * P], q % 2 == 1 and r % 2 == 1)

        vj_codes, vj_scales = quantize(v_j[:].rearrange("p t d r -> p (t d r)"), "vj", E4M3, tag="shift3")
        g_p = tile([P, PACK, N], BF16, "g_p", tag="v_g")
        col_mean = [tile([P, 1], F32, "col_mean%d" % r) for r in range(PACK)]
        part = [tile([P, 1], F32, "part%d" % r) for r in range(PACK)]
        junk = [tile([P, N], BF16, "junk%d" % r) for r in range(PACK)]
        for r in range(PACK):
            nc.scalar.activation(
                junk[r][:, 0:H], c_half(0, r), ACT.Copy, scale=1.0 / N if r < 2 else 1.0 / (N * H), accum_out=part[r][:]
            )
        for r in range(PACK):
            if r < 2:
                nc.vector.tensor_scalar(
                    junk[r][:, H:N], c_half(1, r), 1.0 / N, part[r][:], ALU.mult, ALU.add, accum_out=col_mean[r][:]
                )
            else:
                nc.scalar.activation(
                    junk[r][:, H:N], c_half(1, r), ACT.Identity, scale=1.0 / N, bias=part[r][:], accum_out=col_mean[r][:]
                )
        g_j = tile([P, N, PACK], BF16, "g_j", tag="v_d")
        out_rows = out_0.rearrange("(p t) c -> p t c", t=PACK)
        du_lo = [
            [tile([P, H], F32, "du%d_%d" % (t, h), tag=None) for h in range(2)]
            for t in range(2)
        ]
        du_banks = (("A0", "A1"), ("A2", "A3"))

        def second_product(t, cols, dst):
            rows = slice(t * P, (t + 1) * P)
            nc.tensor.matmul_mx(
                dst, lhsT=vj_codes[:, rows].bitcast(E4M3), lhsT_scale=vj_scales[:, rows],
                rhs=g_codes[:, cols].bitcast(E5M2), rhs_scale=g_scales[:, cols], start=True, stop=True,
            )

        def places(t, h):
            return out_win[t][:].indirect(item_list[:, h * H // 16 : (h + 1) * H // 16])

        du_ps = []
        for h, SHARE in enumerate((144, 256)):
            lo, hi = h * H, (h + 1) * H
            for r in range(PACK):
                nc.vector.scalar_tensor_tensor(
                    g_p[:, r, lo:hi], c_half(h, r), col_mean[r][:], w[r][:, lo:hi], ALU.subtract, ALU.mult
                )
            if SHARE < H:
                nc.scalar.copy(g_j[:, lo + SHARE : hi, :], g_p[:, :, lo + SHARE : hi].rearrange("p r i -> p i r"))
            nc.vector.tensor_copy(g_j[:, lo : lo + SHARE, :], g_p[:, :, lo : lo + SHARE].rearrange("p r i -> p i r"))
            nc.vector.quantize_mx(
                out=g_codes[:, lo:hi].bitcast(E5M2), scales=g_scales[:, lo:hi],
                in_=g_j[:, lo:hi, :].rearrange("p i r -> p (i r)"),
            )
            banks = [bank("du_ps%d_%d" % (h, k), du_banks[h][k]) for k in range(2)]
            du_ps.append(banks)
            second_product(0, slice(lo, hi), banks[0][:, 0:H])
            second_product(1, slice(lo, hi), banks[1][:, 0:H])
            nc.scalar.copy(du_lo[0][h][:], banks[0][:, 0:H])
            if h == 0:
                nc.scalar.copy(du_lo[1][h][:], banks[1][:, 0:H])
            nc.scalar.activation(places(0, h), du_lo[0][h][:], ACT.Copy)
        hi_ps = [bank("hi_ps%d" % k, "C%d" % k) for k in range(2)]
        for k in range(2):
            second_product(2 + k, slice(0, N), hi_ps[k][:])
        nc.sync.dma_start(out_rows[:, 0, :], out_win[0][:])
        du_hi = [tile([P, N], F32, "du_hi%d" % k, tag=("du_third", "du_last")[k]) for k in range(2)]
        nc.vector.tensor_copy(places(1, 0), du_lo[1][0][:])
        nc.vector.tensor_copy(du_lo[1][1][:], du_ps[1][1][:, 0:H])
        nc.vector.tensor_copy(du_hi[1][:], hi_ps[1][:])
        nc.vector.tensor_copy(places(1, 1), du_lo[1][1][:])
        nc.sync.dma_start(out_rows[:, 1, :], out_win[1][:])
        nc.scalar.copy(du_hi[0][:], hi_ps[0][:])
        for h in range(2):
            nc.scalar.activation(places(2, h), du_hi[0][:, h * H : (h + 1) * H], ACT.Copy)
        nc.scalar.dma_start(out_rows[:, 2, :], out_win[2][:])
        nc.vector.tensor_copy(out_win[3][:].indirect(item_list[:]), du_hi[1][:])
        nc.sync.dma_start(out_rows[:, 3, :], out_win[3][:])

        rounded = [
            tile([P, PACK, hi - lo], BF16, "rounded%d" % lo, tag="du_third" if hi == T else None) for lo, hi in ROUND_COLS
        ]

        def rounded_cols(lo, hi):
            c = [k for k, (first, end) in enumerate(ROUND_COLS) if first <= lo < end][0]
            return rounded[c][:, :, lo - ROUND_COLS[c][0] : hi - ROUND_COLS[c][0]]

        woven = {lo: tile([P, hi - lo, PACK], BF16, "woven%d" % lo) for lo, hi in OUT_COLS}

        def round_plane(eng, t, lo, hi):
            dst, src = rounded_cols(lo, hi)[:, t, :], out_win[t][:, lo:hi]
            if eng == "gpsimd":
                nc.gpsimd.tensor_scalar(dst, src, 1.0, 0.0, ALU.mult, ALU.add)
            elif eng == "scalar":
                nc.scalar.copy(dst, src)
            else:
                nc.vector.tensor_copy(dst, src)

        def weave(eng, lo, hi):
            dst = woven[lo][:].rearrange("p (c i) t -> p c t i", i=PACK)
            src = rounded_cols(lo, hi).rearrange("p t (c i) -> p c t i", i=PACK)
            if eng == "scalar":
                nc.scalar.copy(woven[lo][:], rounded_cols(lo, hi).rearrange("p t c -> p c t"))
            else:
                nc.vector.tensor_copy(dst, src)

        out_codes = tile([P, T], U32, "out_codes")
        out_scales = tile([P, T // 2], U8, "out_scales")
        words = out_1[0].rearrange("p c l -> p (c l)").bitcast(I32)

        def quantize_out(lo, hi):
            nc.vector.quantize_mx(
                out=out_codes[:, lo:hi].bitcast(E4M3),
                scales=out_scales[PACK * (lo // (T // 2)) : P, lo % (T // 2) : lo % (T // 2) + hi - lo],
                in_=woven[lo][:].rearrange("p c t -> p (c t)"),
            )
            nc.sync.dma_start(words[:, lo:hi], out_codes[:, lo:hi].bitcast(I32))

        round_plane("gpsimd", 0, 0, 512)
        round_plane("gpsimd", 0, 512, 1152)
        for lo, hi in ROUND_COLS[:2]:
            round_plane("gpsimd", 1, lo, hi)
        for lo, hi in ROUND_COLS[:2]:
            round_plane("vector", 3, lo, hi)
        round_plane("scalar", 2, 0, 512)
        round_plane("scalar", 0, 1152, 1536)
        round_plane("scalar", 2, 512, 1536)
        for t in range(PACK):
            round_plane("scalar", t, *ROUND_COLS[2])
        for lo, hi in OUT_COLS:
            weave("vector" if hi <= 1536 else "scalar", lo, hi)
        for lo, hi in OUT_COLS:
            quantize_out(lo, hi)
        scale_rows = out_2[0].bitcast(I32).rearrange("(q r) (a c) -> q a r c", r=PACK, a=2)
        for Q in range(PACK):
            (nc.sync if Q % 2 == 0 else nc.scalar).dma_start(scale_rows[Q], out_scales[32 * Q : 32 * Q + 2 * PACK, :].bitcast(I32))
